import numpy as np
import ml_dtypes


def mxq(x, axis, fmt="e4m3"):
    dtype, down = {"e4m3": (ml_dtypes.float8_e4m3fn, 7), "e5m2": (ml_dtypes.float8_e5m2, 14)}[fmt]
    v = np.moveaxis(np.asarray(x, np.float32).astype(ml_dtypes.bfloat16).astype(np.float64), axis, -1)
    blocks = v.reshape(v.shape[:-1] + (-1, 32))
    amax = np.abs(blocks).max(-1, keepdims=True)
    byte = np.maximum(np.where(amax > 0, np.frexp(amax)[1] - 1 + 127, 0) - down, 1)
    scale = np.exp2(byte - 127.0)
    codes = (blocks / scale).astype(np.float32).astype(dtype).astype(np.float64)
    return np.moveaxis((codes * scale).reshape(v.shape), -1, axis)


WIDE = False


def mx_kscale(k):
    if not WIDE:
        return np.ones(k)
    levels = np.array([10, -10, 5, -5, 0])
    if k % 512:
        return np.exp2(np.random.permutation(np.resize(levels, k // 32))).repeat(32)
    a = np.empty((k // 512, 16))
    for p in range(k // 512):
        a[p, :8] = np.random.permutation(np.resize(levels, 8))
        for g in range(8):
            far = levels[np.abs(levels - a[p, g]) >= 10]
            a[p, g + 8] = far[np.random.randint(len(far))]
    return np.exp2(a.ravel()).repeat(32)


def f64(x):
    return np.asarray(x).astype(np.float64)


def striped(idx):
    return np.tile(idx.reshape(-1, 16).T, (8, 1)).astype(np.uint16)


def unstriped(offs):
    return offs[:16].T.reshape(-1).astype(np.int64)


E2M1 = np.array([0.0, 0.5, 1.0, 1.5, 2.0, 3.0, 4.0, 6.0, -0.0, -0.5, -1.0, -1.5, -2.0, -3.0, -4.0, -6.0])


def pack_weight(w, fmt):
    k, n = w.shape
    w = f64(np.asarray(w, np.float32).astype(ml_dtypes.bfloat16)).reshape(k // 32, 32, n)
    amax = np.abs(w).max(1)
    if fmt == "e4m3":
        byte = np.frexp(amax)[1] - 1 + 127 - 7
    else:
        mant, ex = np.frexp(amax / 6.0)
        byte = np.where(mant > 0.5, ex, ex - 1) + 127
    byte = np.clip(np.where(amax > 0, byte, 1), 1, 254)
    scaled = (w * np.exp2(127.0 - byte)[:, None, :]).reshape(k, n).astype(np.float32)
    by_word = np.ascontiguousarray(scaled.reshape(k // 512, 128, 4, n).transpose(0, 1, 3, 2))
    if fmt == "e4m3":
        words = by_word.astype(ml_dtypes.float8_e4m3fn).view(np.uint8)
    else:
        c = by_word.astype(ml_dtypes.float4_e2m1fn).view(np.uint8) & 0xF
        words = (c[..., 0::2] | (c[..., 1::2] << 4)).reshape(k // 512, 128, 2 * n)
    return np.ascontiguousarray(words), np.ascontiguousarray(byte.astype(np.uint8).reshape(k // 512, 16, n))


def unpack_weight(words, scales, fmt):
    g, _, n = scales.shape
    words = np.ascontiguousarray(words).reshape(g, 128, n, -1)
    if fmt == "e4m3":
        vals = words.view(ml_dtypes.float8_e4m3fn).astype(np.float64)
    else:
        nib = np.empty((g, 128, n, 4), np.uint8)
        nib[..., 0::2] = words & 0xF
        nib[..., 1::2] = words >> 4
        vals = E2M1[nib]
    vals = vals * np.repeat(np.exp2(scales.astype(np.float64) - 127.0), 8, axis=1)[..., None]
    return vals.transpose(0, 1, 3, 2).reshape(g * 512, n)


def pack_table4(v):
    words, scales = pack_weight(v, "e2m1")
    g, t = words.shape[0] // 2, v.shape[1]
    words = words.reshape(g, 2, 128, t, 2).transpose(0, 2, 3, 1, 4)
    return np.concatenate([words.reshape(g, -1), scales.reshape(g, -1)], axis=1)


def unpack_table4(tab):
    g, t = tab.shape[0], tab.shape[1] // 544
    words = tab[:, :512 * t].reshape(g, 128, t, 2, 2).transpose(0, 3, 1, 2, 4).reshape(2 * g, 128, 2 * t)
    return unpack_weight(words, tab[:, 512 * t:].reshape(2 * g, 16, t), "e2m1")


def silu(v):
    return v / (1.0 + np.exp(-np.maximum(v, -700.0)))


K, M, T, S = 1024, 128, 2048, 1024


def setup_inputs():
    n = np.random.standard_normal
    s = mx_kscale(K)[:, None]
    return {
        "tab": pack_table4(n((K, T)) * s),
        "w": (n((K, M)) / np.sqrt(K) / s).astype(np.float32),
        "b": (0.3 * n(128)).astype(np.float32),
        "offs": striped(np.random.permutation(T)[:S]),
    }


def reference(tab, w, b, offs):
    tab_ = unpack_table4(tab)[:, unstriped(offs)]
    w_ = mxq(f64(w), 0, "e4m3")
    y = tab_.T @ w_
    return silu(y + f64(b)[None, :])

@@ -1,0 +1,133 @@
+import concourse.mybir as mybir
+from concourse.masks import make_identity
+
+K, M, T, S = 1024, 128, 2048, 1024
+FLOPS = 2 * K * M * S
+
+F32 = mybir.dt.float32
+BF16 = mybir.dt.bfloat16
+I32 = mybir.dt.int32
+U32 = mybir.dt.uint32
+U16 = mybir.dt.uint16
+U8 = mybir.dt.uint8
+FP8X4 = mybir.dt.float8_e4m3fn_x4
+FP4X4 = mybir.dt.float4_e2m1fn_x4
+SILU = mybir.ActivationFunctionType.Silu
+COPY = mybir.ActivationFunctionType.Copy
+ADD = mybir.AluOpType.add
+
+P = 128
+WORD_BYTES = 512 * T
+BLOCKS = ((0, 256), (256, 256), (512, 256), (768, 256))
+
+
+def tile_list_tab4_tm_silu_kernel(tc, tab, w, b, offs, out):
+    nc = tc.nc
+    with (
+        tc.tile_pool(name="held", bufs=1) as held,
+        tc.psum_pool(name="psum", bufs=1) as psum,
+    ):
+        offsets = held.tile([P, S // 16], U16, name="offsets")
+        scale_tab = held.tile([P, T], U8, name="scale_tab", align_bytes=64)
+        word_tab = held.tile([P, T], I32, name="word_tab", align_bytes=64)
+        w_raw = held.tile([P, 2, 4, M], F32, name="w_raw", align_bytes=64)
+        w_grp = held.tile([P, 2, M, 4], BF16, name="w_grp", align_bytes=64)
+        w_codes = held.tile([P, 2, M], U32, name="w_codes", align_bytes=64)
+        w_scales = held.tile([P, 2, M], U8, name="w_scales", align_bytes=64)
+        b_col = held.tile([P, 1], F32, name="b_col")
+        b_row = held.tile([P, M], F32, name="b_row", align_bytes=64)
+        ident = held.tile([P, P], F32, name="ident", align_bytes=64)
+        warm = held.tile([P, 1], F32, name="warm")
+        picked = held.tile([P, S], U8, name="picked", align_bytes=64)
+        plane0 = held.tile([P, S], U8, name="plane0", align_bytes=64)
+        plane1 = held.tile([P, S], U8, name="plane1", align_bytes=64)
+        planes = (plane0, plane1)
+
+        nc.sync.dma_start(offsets[:], offs)
+        scale_rows = tab[0, WORD_BYTES : WORD_BYTES + 32 * T].rearrange("(q t) -> q t", t=T)
+        nc.sync.dma_start(scale_tab[0:32, :].bitcast(I32), scale_rows.bitcast(I32))
+        nc.sync.dma_start(word_tab[:], tab[0, 0:WORD_BYTES].rearrange("(p x) -> p x", p=P).bitcast(I32))
+        nc.sync.dma_start(w_raw[:].rearrange("p h i n -> p h (i n)"), w.rearrange("(h p i) n -> p h (i n)", h=2, i=4))
+        nc.gpsimd.dma_start(b_col[:], b.rearrange("(p o) -> p o", o=1))
+        nc.vector.memset(scale_tab[32:64, :].bitcast(I32), 0)
+        nc.vector.memset(scale_tab[64:128, :].bitcast(I32), 0)
+        nc.vector.memset(warm[:], 0.0)
+        nc.scalar.activation(warm[:], warm[:], SILU)
+
+        nc.vector.tensor_copy(picked[:], scale_tab[:].indirect(offsets[:]))
+        for h in range(2):
+            for q in range(4):
+                queue = nc.sync if h == 0 else nc.gpsimd if q == 0 else nc.scalar
+                queue.dma_start(planes[h][32 * q : 32 * q + 4, :].bitcast(I32), picked[16 * h + 4 * q : 16 * h + 4 * q + 4, :].bitcast(I32))
+
+        for h in range(2):
+            nc.scalar.activation(w_grp[:, h], w_raw[:, h].rearrange("p i n -> p n i"), COPY)
+
+        make_identity(nc, ident[:])
+        b_bank = psum.tile([P, M], F32, name="b_bank", tag="acc0")
+        nc.tensor.transpose(b_bank[:], b_col[:].to_broadcast([P, M]), ident[:])
+        nc.scalar.copy(b_row[:], b_bank[:])
+
+        words = []
+        codes = []
+        for t0, n in BLOCKS:
+            g = held.tile([P, n], U32, name=f"g{t0}", align_bytes=64)
+            words.append(g)
+            cd = held.tile([P, 2, n], U16, name=f"cd{t0}", align_bytes=64)
+            codes.append(cd)
+
+        def gather(s):
+            t0, n = BLOCKS[s]
+            nc.vector.tensor_copy(words[s][:], word_tab[:].bitcast(U32).indirect(offsets[:, t0 // 16 : (t0 + n) // 16]))
+
+        def part(s, a, n):
+            nc.vector.tensor_copy(codes[s][:, :, a : a + n], words[s][:, a : a + n].bitcast(U16).rearrange("p (t h) -> p h t", h=2))
+
+        def table_operand(s, h, a, n):
+            t0, total = BLOCKS[s]
+            raw = codes[s][:].rearrange("p h t -> p (h t)").bitcast(U8)
+            b0 = 2 * (h * total + a)
+            return raw[:, b0 : b0 + 2 * n].bitcast(FP4X4), planes[h][:, t0 + a : t0 + a + n]
+
+        def multiply(s, a, n):
+            t0, total = BLOCKS[s]
+            acc = psum.tile([P, n // P, M], F32, name=f"acc{t0 + a}", tag=f"acc{t0 + a}")
+            for c in range(n // P):
+                for h in range(2):
+                    codes_ap, scales_ap = table_operand(s, h, a + c * P, P)
+                    nc.tensor.matmul_mx(out=acc[:, c, :], lhsT=codes_ap, lhsT_scale=scales_ap,
+                                        rhs=w_codes[:, h, :].bitcast(FP8X4), rhs_scale=w_scales[:, h, :], start=(h == 0), stop=(h == 1))
+            return acc
+
+        def finish(s, a, n, acc):
+            t0, total = BLOCKS[s]
+            y = held.tile([P, n // P, M], F32, name=f"y{t0 + a}", align_bytes=64)
+            o = held.tile([P, n // P, M], F32, name=f"o{t0 + a}", align_bytes=64)
+            nc.vector.tensor_tensor(y[:], acc[:], b_row[:].unsqueeze(1).to_broadcast([P, n // P, M]), ADD)
+            nc.scalar.activation(o[:], y[:], SILU)
+            nc.sync.dma_start(out[t0 + a : t0 + a + n, :].rearrange("(c p) n -> p c n", p=P), o[:])
+
+        gather(0)
+        part(0, 0, 256)
+        gather(1)
+        part(1, 0, 256)
+        nc.vector.quantize_mx(
+            out=w_codes[:].rearrange("p h n -> p (h n)").bitcast(FP8X4),
+            scales=w_scales[:].rearrange("p h n -> p (h n)"),
+            in_=w_grp[:].rearrange("p h n i -> p (h n i)"),
+        )
+        acc0 = multiply(0, 0, 256)
+        acc1 = multiply(1, 0, 256)
+        gather(2)
+        part(2, 0, 256)
+        acc2 = multiply(2, 0, 256)
+        gather(3)
+        finish(0, 0, 256, acc0)
+        part(3, 0, P)
+        acc3a = multiply(3, 0, P)
+        part(3, P, P)
+        acc3b = multiply(3, P, P)
+        finish(1, 0, 256, acc1)
+        finish(2, 0, 256, acc2)
+        finish(3, 0, P, acc3a)
+        finish(3, P, P, acc3b)

@@ -18,7 +18,7 @@ ADD = mybir.AluOpType.add
 
 P = 128
 WORD_BYTES = 512 * T
-BLOCKS = ((0, 256), (256, 256), (512, 256), (768, 256))
+BLOCK = 256
 
 
 def tile_list_tab4_tm_silu_kernel(tc, tab, w, b, offs, out):
@@ -31,24 +31,23 @@ def tile_list_tab4_tm_silu_kernel(tc, tab, w, b, offs, out):
         scale_tab = held.tile([P, T], U8, name="scale_tab", align_bytes=64)
         word_tab = held.tile([P, T], I32, name="word_tab", align_bytes=64)
         w_raw = held.tile([P, 2, 4, M], F32, name="w_raw", align_bytes=64)
-        w_grp = held.tile([P, 2, M, 4], BF16, name="w_grp", align_bytes=64)
-        w_codes = held.tile([P, 2, M], U32, name="w_codes", align_bytes=64)
-        w_scales = held.tile([P, 2, M], U8, name="w_scales", align_bytes=64)
+        w_grp = [held.tile([P, M, 4], BF16, name=f"w_grp{h}", tag=f"words{2 + h}", align_bytes=64) for h in range(2)]
+        w_codes = [held.tile([P, M], U32, name=f"w_codes{h}", align_bytes=64) for h in range(2)]
+        w_scales = [held.tile([P, M], U8, name=f"w_scales{h}", align_bytes=64) for h in range(2)]
         b_col = held.tile([P, 1], F32, name="b_col")
         b_row = held.tile([P, M], F32, name="b_row", align_bytes=64)
         ident = held.tile([P, P], F32, name="ident", align_bytes=64)
         warm = held.tile([P, 1], F32, name="warm")
         picked = held.tile([P, S], U8, name="picked", align_bytes=64)
-        plane0 = held.tile([P, S], U8, name="plane0", align_bytes=64)
-        plane1 = held.tile([P, S], U8, name="plane1", align_bytes=64)
-        planes = (plane0, plane1)
+        planes = [held.tile([P, S], U8, name=f"plane{h}", align_bytes=64) for h in range(2)]
 
-        nc.sync.dma_start(offsets[:], offs)
         scale_rows = tab[0, WORD_BYTES : WORD_BYTES + 32 * T].rearrange("(q t) -> q t", t=T)
         nc.sync.dma_start(scale_tab[0:32, :].bitcast(I32), scale_rows.bitcast(I32))
+        nc.sync.dma_start(offsets[:], offs)
         nc.sync.dma_start(word_tab[:], tab[0, 0:WORD_BYTES].rearrange("(p x) -> p x", p=P).bitcast(I32))
         nc.sync.dma_start(w_raw[:].rearrange("p h i n -> p h (i n)"), w.rearrange("(h p i) n -> p h (i n)", h=2, i=4))
         nc.gpsimd.dma_start(b_col[:], b.rearrange("(p o) -> p o", o=1))
+
         nc.vector.memset(scale_tab[32:64, :].bitcast(I32), 0)
         nc.vector.memset(scale_tab[64:128, :].bitcast(I32), 0)
         nc.vector.memset(warm[:], 0.0)
@@ -57,77 +56,63 @@ def tile_list_tab4_tm_silu_kernel(tc, tab, w, b, offs, out):
         nc.vector.tensor_copy(picked[:], scale_tab[:].indirect(offsets[:]))
         for h in range(2):
             for q in range(4):
-                queue = nc.sync if h == 0 else nc.gpsimd if q == 0 else nc.scalar
+                queue = nc.sync if q % 2 == 0 else nc.scalar
                 queue.dma_start(planes[h][32 * q : 32 * q + 4, :].bitcast(I32), picked[16 * h + 4 * q : 16 * h + 4 * q + 4, :].bitcast(I32))
 
         for h in range(2):
-            nc.scalar.activation(w_grp[:, h], w_raw[:, h].rearrange("p i n -> p n i"), COPY)
+            nc.scalar.activation(w_grp[h][:], w_raw[:, h].rearrange("p i n -> p n i"), COPY)
 
         make_identity(nc, ident[:])
         b_bank = psum.tile([P, M], F32, name="b_bank", tag="acc0")
         nc.tensor.transpose(b_bank[:], b_col[:].to_broadcast([P, M]), ident[:])
         nc.scalar.copy(b_row[:], b_bank[:])
 
-        words = []
-        codes = []
-        for t0, n in BLOCKS:
-            g = held.tile([P, n], U32, name=f"g{t0}", align_bytes=64)
-            words.append(g)
-            cd = held.tile([P, 2, n], U16, name=f"cd{t0}", align_bytes=64)
-            codes.append(cd)
+        def quantize(h):
+            nc.vector.quantize_mx(out=w_codes[h][:].bitcast(FP8X4), scales=w_scales[h][:], in_=w_grp[h][:].rearrange("p n i -> p (n i)"))
 
         def gather(s):
-            t0, n = BLOCKS[s]
-            nc.vector.tensor_copy(words[s][:], word_tab[:].bitcast(U32).indirect(offsets[:, t0 // 16 : (t0 + n) // 16]))
+            g = held.tile([P, BLOCK], U32, name=f"words{s}", tag=f"words{s}", align_bytes=64)
+            t0 = s * BLOCK
+            nc.vector.tensor_copy(g[:], word_tab[:].bitcast(U32).indirect(offsets[:, t0 // 16 : (t0 + BLOCK) // 16]))
+            return g
 
-        def part(s, a, n):
-            nc.vector.tensor_copy(codes[s][:, :, a : a + n], words[s][:, a : a + n].bitcast(U16).rearrange("p (t h) -> p h t", h=2))
+        def part(g, t0, n):
+            cd = held.tile([P, 2, n], U16, name=f"codes{t0}", align_bytes=64)
+            a = t0 % BLOCK
+            nc.vector.tensor_copy(cd[:], g[:, a : a + n].bitcast(U16).rearrange("p (t h) -> p h t", h=2))
+            return cd
 
-        def table_operand(s, h, a, n):
-            t0, total = BLOCKS[s]
-            raw = codes[s][:].rearrange("p h t -> p (h t)").bitcast(U8)
-            b0 = 2 * (h * total + a)
-            return raw[:, b0 : b0 + 2 * n].bitcast(FP4X4), planes[h][:, t0 + a : t0 + a + n]
+        def one_pass(acc, cd, t0, c, h):
+            n = cd.shape[2]
+            raw = cd[:].rearrange("p h t -> p (h t)").bitcast(U8)
+            b0 = 2 * (h * n + c * P)
+            nc.tensor.matmul_mx(out=acc[:, c, :], lhsT=raw[:, b0 : b0 + 2 * P].bitcast(FP4X4), lhsT_scale=planes[h][:, t0 + c * P : t0 + (c + 1) * P],
+                                rhs=w_codes[h][:].bitcast(FP8X4), rhs_scale=w_scales[h][:], start=(h == 0), stop=(h == 1))
 
-        def multiply(s, a, n):
-            t0, total = BLOCKS[s]
-            acc = psum.tile([P, n // P, M], F32, name=f"acc{t0 + a}", tag=f"acc{t0 + a}")
+        def bank(t0, n):
+            return psum.tile([P, n // P, M], F32, name=f"acc{t0}", tag=f"acc{t0}")
+
+        def multiply(cd, t0, n):
+            acc = bank(t0, n)
             for c in range(n // P):
                 for h in range(2):
-                    codes_ap, scales_ap = table_operand(s, h, a + c * P, P)
-                    nc.tensor.matmul_mx(out=acc[:, c, :], lhsT=codes_ap, lhsT_scale=scales_ap,
-                                        rhs=w_codes[:, h, :].bitcast(FP8X4), rhs_scale=w_scales[:, h, :], start=(h == 0), stop=(h == 1))
+                    one_pass(acc, cd, t0, c, h)
             return acc
 
-        def finish(s, a, n, acc):
-            t0, total = BLOCKS[s]
-            y = held.tile([P, n // P, M], F32, name=f"y{t0 + a}", align_bytes=64)
-            o = held.tile([P, n // P, M], F32, name=f"o{t0 + a}", align_bytes=64)
+        def finish(t0, n, acc, queue=nc.sync):
+            y = held.tile([P, n // P, M], F32, name=f"y{t0}", align_bytes=64)
+            o = held.tile([P, n // P, M], F32, name=f"o{t0}", align_bytes=64)
             nc.vector.tensor_tensor(y[:], acc[:], b_row[:].unsqueeze(1).to_broadcast([P, n // P, M]), ADD)
             nc.scalar.activation(o[:], y[:], SILU)
-            nc.sync.dma_start(out[t0 + a : t0 + a + n, :].rearrange("(c p) n -> p c n", p=P), o[:])
+            queue.dma_start(out[t0 : t0 + n, :].rearrange("(c p) n -> p c n", p=P), o[:])
 
-        gather(0)
-        part(0, 0, 256)
-        gather(1)
-        part(1, 0, 256)
-        nc.vector.quantize_mx(
-            out=w_codes[:].rearrange("p h n -> p (h n)").bitcast(FP8X4),
-            scales=w_scales[:].rearrange("p h n -> p (h n)"),
-            in_=w_grp[:].rearrange("p h n i -> p (h n i)"),
-        )
-        acc0 = multiply(0, 0, 256)
-        acc1 = multiply(1, 0, 256)
-        gather(2)
-        part(2, 0, 256)
-        acc2 = multiply(2, 0, 256)
-        gather(3)
-        finish(0, 0, 256, acc0)
-        part(3, 0, P)
-        acc3a = multiply(3, 0, P)
-        part(3, P, P)
-        acc3b = multiply(3, P, P)
-        finish(1, 0, 256, acc1)
-        finish(2, 0, 256, acc2)
-        finish(3, 0, P, acc3a)
-        finish(3, P, P, acc3b)
+        cd0 = part(gather(0), 0, BLOCK)
+        cd1 = part(gather(1), BLOCK, BLOCK)
+        quantize(0)
+        cd2 = part(gather(2), 2 * BLOCK, BLOCK)
+        quantize(1)
+        cd3 = part(gather(3), 3 * BLOCK, BLOCK)
+        accs = [multiply(cd, s * BLOCK, BLOCK) for s, cd in enumerate((cd0, cd1, cd2, cd3))]
+        for s in range(3):
+            finish(s * BLOCK, BLOCK, accs[s])
+        finish(3 * BLOCK, BLOCK, accs[3], nc.scalar)

@@ -19,19 +19,21 @@ ADD = mybir.AluOpType.add
 P = 128
 WORD_BYTES = 512 * T
 BLOCK = 256
+HALF_W = 4 * M * 4
 
 
 def tile_list_tab4_tm_silu_kernel(tc, tab, w, b, offs, out):
     nc = tc.nc
     with (
         tc.tile_pool(name="held", bufs=1) as held,
+        tc.tile_pool(name="reused", bufs=1) as reused,
         tc.psum_pool(name="psum", bufs=1) as psum,
     ):
         offsets = held.tile([P, S // 16], U16, name="offsets")
         scale_tab = held.tile([P, T], U8, name="scale_tab", align_bytes=64)
         word_tab = held.tile([P, T], I32, name="word_tab", align_bytes=64)
-        w_raw = held.tile([P, 2, 4, M], F32, name="w_raw", align_bytes=64)
-        w_grp = [held.tile([P, M, 4], BF16, name=f"w_grp{h}", tag=f"words{2 + h}", align_bytes=64) for h in range(2)]
+        w_raw = [reused.tile([P, 4, M], F32, name=f"w_raw{h}", align_bytes=64, offset=h * HALF_W) for h in range(2)]
+        w_grp = [held.tile([P, M, 4], BF16, name=f"w_grp{h}", align_bytes=64) for h in range(2)]
         w_codes = [held.tile([P, M], U32, name=f"w_codes{h}", align_bytes=64) for h in range(2)]
         w_scales = [held.tile([P, M], U8, name=f"w_scales{h}", align_bytes=64) for h in range(2)]
         b_col = held.tile([P, 1], F32, name="b_col")
@@ -45,74 +47,84 @@ def tile_list_tab4_tm_silu_kernel(tc, tab, w, b, offs, out):
         nc.sync.dma_start(scale_tab[0:32, :].bitcast(I32), scale_rows.bitcast(I32))
         nc.sync.dma_start(offsets[:], offs)
         nc.sync.dma_start(word_tab[:], tab[0, 0:WORD_BYTES].rearrange("(p x) -> p x", p=P).bitcast(I32))
-        nc.sync.dma_start(w_raw[:].rearrange("p h i n -> p h (i n)"), w.rearrange("(h p i) n -> p h (i n)", h=2, i=4))
-        nc.gpsimd.dma_start(b_col[:], b.rearrange("(p o) -> p o", o=1))
-
+        nc.sync.dma_start(b_col[:], b.rearrange("(p o) -> p o", o=1))
+        for h in range(2):
+            nc.sync.dma_start(w_raw[h][:].rearrange("p i n -> p (i n)"), w[512 * h : 512 * (h + 1), :].rearrange("(p i) n -> p (i n)", i=4))
         nc.vector.memset(scale_tab[32:64, :].bitcast(I32), 0)
         nc.vector.memset(scale_tab[64:128, :].bitcast(I32), 0)
         nc.vector.memset(warm[:], 0.0)
         nc.scalar.activation(warm[:], warm[:], SILU)
 
+        make_identity(nc, ident[:])
+        b_bank = psum.tile([P, M], F32, name="b_bank")
+        nc.tensor.transpose(b_bank[:], b_col[:].to_broadcast([P, M]), ident[:])
+        nc.scalar.copy(b_row[:], b_bank[:])
+
         nc.vector.tensor_copy(picked[:], scale_tab[:].indirect(offsets[:]))
         for h in range(2):
             for q in range(4):
-                queue = nc.sync if q % 2 == 0 else nc.scalar
+                queue = nc.scalar if q == 1 or (h, q) == (0, 3) else nc.sync
                 queue.dma_start(planes[h][32 * q : 32 * q + 4, :].bitcast(I32), picked[16 * h + 4 * q : 16 * h + 4 * q + 4, :].bitcast(I32))
 
         for h in range(2):
-            nc.scalar.activation(w_grp[h][:], w_raw[:, h].rearrange("p i n -> p n i"), COPY)
-
-        make_identity(nc, ident[:])
-        b_bank = psum.tile([P, M], F32, name="b_bank", tag="acc0")
-        nc.tensor.transpose(b_bank[:], b_col[:].to_broadcast([P, M]), ident[:])
-        nc.scalar.copy(b_row[:], b_bank[:])
+            nc.scalar.activation(w_grp[h][:], w_raw[h][:].rearrange("p i n -> p n i"), COPY)
 
         def quantize(h):
             nc.vector.quantize_mx(out=w_codes[h][:].bitcast(FP8X4), scales=w_scales[h][:], in_=w_grp[h][:].rearrange("p n i -> p (n i)"))
 
-        def gather(s):
-            g = held.tile([P, BLOCK], U32, name=f"words{s}", tag=f"words{s}", align_bytes=64)
+        def gather(g, s):
             t0 = s * BLOCK
             nc.vector.tensor_copy(g[:], word_tab[:].bitcast(U32).indirect(offsets[:, t0 // 16 : (t0 + BLOCK) // 16]))
-            return g
 
-        def part(g, t0, n):
-            cd = held.tile([P, 2, n], U16, name=f"codes{t0}", align_bytes=64)
-            a = t0 % BLOCK
-            nc.vector.tensor_copy(cd[:], g[:, a : a + n].bitcast(U16).rearrange("p (t h) -> p h t", h=2))
-            return cd
+        def part(cd, g):
+            nc.vector.tensor_copy(cd[:], g[:].bitcast(U16).rearrange("p (t h) -> p h t", h=2))
 
-        def one_pass(acc, cd, t0, c, h):
-            n = cd.shape[2]
+        def one_pass(acc, cd, t, h):
             raw = cd[:].rearrange("p h t -> p (h t)").bitcast(U8)
-            b0 = 2 * (h * n + c * P)
-            nc.tensor.matmul_mx(out=acc[:, c, :], lhsT=raw[:, b0 : b0 + 2 * P].bitcast(FP4X4), lhsT_scale=planes[h][:, t0 + c * P : t0 + (c + 1) * P],
+            b0 = 2 * (h * BLOCK + (t % 2) * P)
+            nc.tensor.matmul_mx(out=acc, lhsT=raw[:, b0 : b0 + 2 * P].bitcast(FP4X4), lhsT_scale=planes[h][:, t * P : (t + 1) * P],
                                 rhs=w_codes[h][:].bitcast(FP8X4), rhs_scale=w_scales[h][:], start=(h == 0), stop=(h == 1))
 
-        def bank(t0, n):
-            return psum.tile([P, n // P, M], F32, name=f"acc{t0}", tag=f"acc{t0}")
-
-        def multiply(cd, t0, n):
-            acc = bank(t0, n)
-            for c in range(n // P):
-                for h in range(2):
-                    one_pass(acc, cd, t0, c, h)
-            return acc
-
-        def finish(t0, n, acc, queue=nc.sync):
-            y = held.tile([P, n // P, M], F32, name=f"y{t0}", align_bytes=64)
-            o = held.tile([P, n // P, M], F32, name=f"o{t0}", align_bytes=64)
-            nc.vector.tensor_tensor(y[:], acc[:], b_row[:].unsqueeze(1).to_broadcast([P, n // P, M]), ADD)
+        def finish(t0, accs, queue=nc.sync):
+            n = sum(acc.shape[1] for acc in accs)
+            y = held.tile([P, n, M], F32, name=f"y{t0}", align_bytes=64)
+            o = held.tile([P, n, M], F32, name=f"o{t0}", align_bytes=64)
+            c = 0
+            for acc in accs:
+                k = acc.shape[1]
+                nc.vector.tensor_tensor(y[:, c : c + k, :], acc[:], b_row[:].unsqueeze(1).to_broadcast([P, k, M]), ADD)
+                c = c + k
             nc.scalar.activation(o[:], y[:], SILU)
-            queue.dma_start(out[t0 : t0 + n, :].rearrange("(c p) n -> p c n", p=P), o[:])
+            queue.dma_start(out[t0 * P : (t0 + n) * P, :].rearrange("(c p) n -> p c n", p=P), o[:])
 
-        cd0 = part(gather(0), 0, BLOCK)
-        cd1 = part(gather(1), BLOCK, BLOCK)
+        words = [held.tile([P, BLOCK], U32, name=f"words{s}", align_bytes=64) for s in range(2)]
+        codes = [held.tile([P, 2, BLOCK], U16, name=f"codes{s}", align_bytes=64) for s in range(2)]
+        for s in range(2):
+            gather(words[s], s)
+        for s in range(2):
+            part(codes[s], words[s])
         quantize(0)
-        cd2 = part(gather(2), 2 * BLOCK, BLOCK)
+        words.append(reused.tile([P, BLOCK], U32, name="words2", align_bytes=64, offset=0))
+        gather(words[2], 2)
         quantize(1)
-        cd3 = part(gather(3), 3 * BLOCK, BLOCK)
-        accs = [multiply(cd, s * BLOCK, BLOCK) for s, cd in enumerate((cd0, cd1, cd2, cd3))]
-        for s in range(3):
-            finish(s * BLOCK, BLOCK, accs[s])
-        finish(3 * BLOCK, BLOCK, accs[3], nc.scalar)
+        words.append(reused.tile([P, BLOCK], U32, name="words3", align_bytes=64, offset=HALF_W))
+        gather(words[3], 3)
+        codes.append(reused.tile([P, 2, BLOCK], U16, name="codes2", align_bytes=64, offset=HALF_W + 4 * BLOCK))
+        part(codes[2], words[2])
+        codes.append(held.tile([P, 2, BLOCK], U16, name="codes3", align_bytes=64))
+        part(codes[3], words[3])
+
+        early = [psum.tile([P, 1, M], F32, name=f"acc{t}") for t in range(4)]
+        pair = psum.tile([P, 2, M], F32, name="acc4")
+        late = [psum.tile([P, 1, M], F32, name=f"acc{t}") for t in (6, 7)]
+        for h in range(2):
+            for t in range(4):
+                one_pass(early[t][:, 0, :], codes[t // 2], t, h)
+        for t in range(4, 8):
+            for h in range(2):
+                one_pass(pair[:, t - 4, :] if t < 6 else late[t - 6][:, 0, :], codes[t // 2], t, h)
+        finish(0, early[0:2])
+        finish(2, early[2:4])
+        finish(4, [pair])
+        finish(6, late[0:1])
+        finish(7, late[1:2])

@@ -20,6 +20,7 @@ P = 128
 WORD_BYTES = 512 * T
 BLOCK = 256
 HALF_W = 4 * M * 4
+BANK = 512
 
 
 def tile_list_tab4_tm_silu_kernel(tc, tab, w, b, offs, out):
@@ -41,33 +42,39 @@ def tile_list_tab4_tm_silu_kernel(tc, tab, w, b, offs, out):
         ident = held.tile([P, P], F32, name="ident", align_bytes=64)
         warm = held.tile([P, 1], F32, name="warm")
         picked = held.tile([P, S], U8, name="picked", align_bytes=64)
-        planes = [held.tile([P, S], U8, name=f"plane{h}", align_bytes=64) for h in range(2)]
+
+        def load_w(h):
+            nc.sync.dma_start(w_raw[h][:].rearrange("p i n -> p (i n)"), w[512 * h : 512 * (h + 1), :].rearrange("(p i) n -> p (i n)", i=4))
+
+        def interleave(h):
+            nc.scalar.activation(w_grp[h][:], w_raw[h][:].rearrange("p i n -> p n i"), COPY)
 
         scale_rows = tab[0, WORD_BYTES : WORD_BYTES + 32 * T].rearrange("(q t) -> q t", t=T)
         nc.sync.dma_start(scale_tab[0:32, :].bitcast(I32), scale_rows.bitcast(I32))
         nc.sync.dma_start(offsets[:], offs)
+        load_w(0)
         nc.sync.dma_start(word_tab[:], tab[0, 0:WORD_BYTES].rearrange("(p x) -> p x", p=P).bitcast(I32))
-        nc.sync.dma_start(b_col[:], b.rearrange("(p o) -> p o", o=1))
-        for h in range(2):
-            nc.sync.dma_start(w_raw[h][:].rearrange("p i n -> p (i n)"), w[512 * h : 512 * (h + 1), :].rearrange("(p i) n -> p (i n)", i=4))
+        load_w(1)
+        nc.gpsimd.dma_start(b_col[:], b.rearrange("(p o) -> p o", o=1))
         nc.vector.memset(scale_tab[32:64, :].bitcast(I32), 0)
         nc.vector.memset(scale_tab[64:128, :].bitcast(I32), 0)
         nc.vector.memset(warm[:], 0.0)
         nc.scalar.activation(warm[:], warm[:], SILU)
 
         make_identity(nc, ident[:])
-        b_bank = psum.tile([P, M], F32, name="b_bank")
-        nc.tensor.transpose(b_bank[:], b_col[:].to_broadcast([P, M]), ident[:])
-        nc.scalar.copy(b_row[:], b_bank[:])
+        b_bank = psum.tile([P, 3 * BANK], F32, name="b_bank", offset=4 * 4 * BANK)
+        nc.tensor.transpose(b_bank[:, 0:M], b_col[:].to_broadcast([P, M]), ident[:])
+        nc.scalar.copy(b_row[:], b_bank[:, 0:M])
 
+        interleave(0)
+        planes = [reused.tile([P, S], U8, name=f"plane{h}", align_bytes=64, offset=h * S) for h in range(2)]
         nc.vector.tensor_copy(picked[:], scale_tab[:].indirect(offsets[:]))
-        for h in range(2):
-            for q in range(4):
-                queue = nc.scalar if q == 1 or (h, q) == (0, 3) else nc.sync
-                queue.dma_start(planes[h][32 * q : 32 * q + 4, :].bitcast(I32), picked[16 * h + 4 * q : 16 * h + 4 * q + 4, :].bitcast(I32))
+        nc.vector.tensor_copy(planes[0][0:4, :].bitcast(I32), picked[0:4, :].bitcast(I32))
+        for h, q in [(h, q) for h in range(2) for q in range(4)][1:]:
+            queue = nc.scalar if q == 1 or (h, q) == (0, 3) else nc.sync
+            queue.dma_start(planes[h][32 * q : 32 * q + 4, :].bitcast(I32), picked[16 * h + 4 * q : 16 * h + 4 * q + 4, :].bitcast(I32))
 
-        for h in range(2):
-            nc.scalar.activation(w_grp[h][:], w_raw[h][:].rearrange("p i n -> p n i"), COPY)
+        interleave(1)
 
         def quantize(h):
             nc.vector.quantize_mx(out=w_codes[h][:].bitcast(FP8X4), scales=w_scales[h][:], in_=w_grp[h][:].rearrange("p n i -> p (n i)"))
@@ -98,25 +105,22 @@ def tile_list_tab4_tm_silu_kernel(tc, tab, w, b, offs, out):
             queue.dma_start(out[t0 * P : (t0 + n) * P, :].rearrange("(c p) n -> p c n", p=P), o[:])
 
         words = [held.tile([P, BLOCK], U32, name=f"words{s}", align_bytes=64) for s in range(2)]
-        codes = [held.tile([P, 2, BLOCK], U16, name=f"codes{s}", align_bytes=64) for s in range(2)]
+        codes = [held.tile([P, 2, BLOCK], U16, name=f"codes{s}", align_bytes=64) for s in range(4)]
+        quantize(0)
         for s in range(2):
             gather(words[s], s)
         for s in range(2):
             part(codes[s], words[s])
-        quantize(0)
-        words.append(reused.tile([P, BLOCK], U32, name="words2", align_bytes=64, offset=0))
-        gather(words[2], 2)
         quantize(1)
-        words.append(reused.tile([P, BLOCK], U32, name="words3", align_bytes=64, offset=HALF_W))
-        gather(words[3], 3)
-        codes.append(reused.tile([P, 2, BLOCK], U16, name="codes2", align_bytes=64, offset=HALF_W + 4 * BLOCK))
-        part(codes[2], words[2])
-        codes.append(held.tile([P, 2, BLOCK], U16, name="codes3", align_bytes=64))
-        part(codes[3], words[3])
+        for s in range(2, 4):
+            words.append(reused.tile([P, BLOCK], U32, name=f"words{s}", align_bytes=64, offset=HALF_W + 4 * BLOCK * (s - 2)))
+            gather(words[s], s)
+        for s in range(2, 4):
+            part(codes[s], words[s])
 
-        early = [psum.tile([P, 1, M], F32, name=f"acc{t}") for t in range(4)]
-        pair = psum.tile([P, 2, M], F32, name="acc4")
-        late = [psum.tile([P, 1, M], F32, name=f"acc{t}") for t in (6, 7)]
+        early = [psum.tile([P, 1, M], F32, name=f"acc{t}", offset=4 * BANK * t) for t in range(4)]
+        pair = psum.tile([P, 2, M], F32, name="acc4", offset=4 * BANK * 4)
+        late = [psum.tile([P, 1, M], F32, name=f"acc{t}", offset=4 * BANK * (t - 1)) for t in (6, 7)]
         for h in range(2):
             for t in range(4):
                 one_pass(early[t][:, 0, :], codes[t // 2], t, h)

@@ -49,33 +49,6 @@ def tile_list_tab4_tm_silu_kernel(tc, tab, w, b, offs, out):
         def interleave(h):
             nc.scalar.activation(w_grp[h][:], w_raw[h][:].rearrange("p i n -> p n i"), COPY)
 
-        scale_rows = tab[0, WORD_BYTES : WORD_BYTES + 32 * T].rearrange("(q t) -> q t", t=T)
-        nc.sync.dma_start(scale_tab[0:32, :].bitcast(I32), scale_rows.bitcast(I32))
-        nc.sync.dma_start(offsets[:], offs)
-        load_w(0)
-        nc.sync.dma_start(word_tab[:], tab[0, 0:WORD_BYTES].rearrange("(p x) -> p x", p=P).bitcast(I32))
-        load_w(1)
-        nc.gpsimd.dma_start(b_col[:], b.rearrange("(p o) -> p o", o=1))
-        nc.vector.memset(scale_tab[32:64, :].bitcast(I32), 0)
-        nc.vector.memset(scale_tab[64:128, :].bitcast(I32), 0)
-        nc.vector.memset(warm[:], 0.0)
-        nc.scalar.activation(warm[:], warm[:], SILU)
-
-        make_identity(nc, ident[:])
-        b_bank = psum.tile([P, 3 * BANK], F32, name="b_bank", offset=4 * 4 * BANK)
-        nc.tensor.transpose(b_bank[:, 0:M], b_col[:].to_broadcast([P, M]), ident[:])
-        nc.scalar.copy(b_row[:], b_bank[:, 0:M])
-
-        interleave(0)
-        planes = [reused.tile([P, S], U8, name=f"plane{h}", align_bytes=64, offset=h * S) for h in range(2)]
-        nc.vector.tensor_copy(picked[:], scale_tab[:].indirect(offsets[:]))
-        nc.vector.tensor_copy(planes[0][0:4, :].bitcast(I32), picked[0:4, :].bitcast(I32))
-        for h, q in [(h, q) for h in range(2) for q in range(4)][1:]:
-            queue = nc.scalar if q == 1 or (h, q) == (0, 3) else nc.sync
-            queue.dma_start(planes[h][32 * q : 32 * q + 4, :].bitcast(I32), picked[16 * h + 4 * q : 16 * h + 4 * q + 4, :].bitcast(I32))
-
-        interleave(1)
-
         def quantize(h):
             nc.vector.quantize_mx(out=w_codes[h][:].bitcast(FP8X4), scales=w_scales[h][:], in_=w_grp[h][:].rearrange("p n i -> p (n i)"))
 
@@ -104,9 +77,36 @@ def tile_list_tab4_tm_silu_kernel(tc, tab, w, b, offs, out):
             nc.scalar.activation(o[:], y[:], SILU)
             queue.dma_start(out[t0 * P : (t0 + n) * P, :].rearrange("(c p) n -> p c n", p=P), o[:])
 
+        scale_rows = tab[0, WORD_BYTES : WORD_BYTES + 32 * T].rearrange("(q t) -> q t", t=T)
+        nc.sync.dma_start(scale_tab[0:32, :].bitcast(I32), scale_rows.bitcast(I32))
+        nc.sync.dma_start(offsets[:], offs)
+        load_w(0)
+        nc.sync.dma_start(word_tab[:], tab[0, 0:WORD_BYTES].rearrange("(p x) -> p x", p=P).bitcast(I32))
+        load_w(1)
+        nc.gpsimd.dma_start(b_col[:], b.rearrange("(p o) -> p o", o=1))
+        nc.vector.memset(scale_tab[32:64, :].bitcast(I32), 0)
+        nc.vector.memset(scale_tab[64:128, :].bitcast(I32), 0)
+        nc.vector.memset(warm[:], 0.0)
+        nc.scalar.activation(warm[:], warm[:], SILU)
+
+        make_identity(nc, ident[:])
+        b_bank = psum.tile([P, 7 * BANK], F32, name="b_bank", offset=0)
+        nc.tensor.transpose(b_bank[:, 0:M], b_col[:].to_broadcast([P, M]), ident[:])
+        nc.scalar.copy(b_row[:], b_bank[:, 0:M])
+
+        interleave(0)
+        planes = [reused.tile([P, S], U8, name=f"plane{h}", align_bytes=64, offset=h * S) for h in range(2)]
+        nc.vector.tensor_copy(picked[:], scale_tab[:].indirect(offsets[:]))
+        quantize(0)
+        nc.vector.tensor_copy(planes[0][0:4, :].bitcast(I32), picked[0:4, :].bitcast(I32))
+        for h, q in [(h, q) for h in range(2) for q in range(4)][1:]:
+            queue = nc.scalar if q == 1 or (h, q) == (0, 3) else nc.sync
+            queue.dma_start(planes[h][32 * q : 32 * q + 4, :].bitcast(I32), picked[16 * h + 4 * q : 16 * h + 4 * q + 4, :].bitcast(I32))
+
+        interleave(1)
+
         words = [held.tile([P, BLOCK], U32, name=f"words{s}", align_bytes=64) for s in range(2)]
         codes = [held.tile([P, 2, BLOCK], U16, name=f"codes{s}", align_bytes=64) for s in range(4)]
-        quantize(0)
         for s in range(2):
             gather(words[s], s)
         for s in range(2):

@@ -59,11 +59,14 @@ def tile_list_tab4_tm_silu_kernel(tc, tab, w, b, offs, out):
         def part(cd, g):
             nc.vector.tensor_copy(cd[:], g[:].bitcast(U16).rearrange("p (t h) -> p h t", h=2))
 
-        def one_pass(acc, cd, t, h):
+        def part_half(cd, g, c):
+            nc.vector.tensor_copy(cd[:, :, c * P : (c + 1) * P], g[:, c * P : (c + 1) * P].bitcast(U16).rearrange("p (t h) -> p h t", h=2))
+
+        def one_pass(acc, cd, t, h, start, stop):
             raw = cd[:].rearrange("p h t -> p (h t)").bitcast(U8)
             b0 = 2 * (h * BLOCK + (t % 2) * P)
             nc.tensor.matmul_mx(out=acc, lhsT=raw[:, b0 : b0 + 2 * P].bitcast(FP4X4), lhsT_scale=planes[h][:, t * P : (t + 1) * P],
-                                rhs=w_codes[h][:].bitcast(FP8X4), rhs_scale=w_scales[h][:], start=(h == 0), stop=(h == 1))
+                                rhs=w_codes[h][:].bitcast(FP8X4), rhs_scale=w_scales[h][:], start=start, stop=stop)
 
         def finish(t0, accs, queue=nc.sync):
             n = sum(acc.shape[1] for acc in accs)
@@ -105,30 +108,34 @@ def tile_list_tab4_tm_silu_kernel(tc, tab, w, b, offs, out):
 
         interleave(1)
 
-        words = [held.tile([P, BLOCK], U32, name=f"words{s}", align_bytes=64) for s in range(2)]
-        codes = [held.tile([P, 2, BLOCK], U16, name=f"codes{s}", align_bytes=64) for s in range(4)]
+        words = [held.tile([P, BLOCK], U32, name="words0", align_bytes=64), reused.tile([P, BLOCK], U32, name="words1", align_bytes=64, offset=2 * HALF_W)]
+        codes = [reused.tile([P, 2, BLOCK], U16, name="codes0", align_bytes=64, offset=2 * HALF_W + 4 * BLOCK)]
         for s in range(2):
             gather(words[s], s)
-        for s in range(2):
-            part(codes[s], words[s])
+        part(codes[0], words[0])
         quantize(1)
-        for s in range(2, 4):
-            words.append(reused.tile([P, BLOCK], U32, name=f"words{s}", align_bytes=64, offset=HALF_W + 4 * BLOCK * (s - 2)))
-            gather(words[s], s)
-        for s in range(2, 4):
-            part(codes[s], words[s])
+        words.append(reused.tile([P, BLOCK], U32, name="words2", align_bytes=64, offset=HALF_W))
+        gather(words[2], 2)
+        codes.append(reused.tile([P, 2, BLOCK], U16, name="codes1", align_bytes=64, offset=HALF_W + 4 * BLOCK))
+        part(codes[1], words[1])
+        codes.append(held.tile([P, 2, BLOCK], U16, name="codes2", align_bytes=64))
+        part(codes[2], words[2])
+        words.append(reused.tile([P, BLOCK], U32, name="words3", align_bytes=64, offset=2 * HALF_W))
+        gather(words[3], 3)
 
-        early = [psum.tile([P, 1, M], F32, name=f"acc{t}", offset=4 * BANK * t) for t in range(4)]
-        pair = psum.tile([P, 2, M], F32, name="acc4", offset=4 * BANK * 4)
-        late = [psum.tile([P, 1, M], F32, name=f"acc{t}", offset=4 * BANK * (t - 1)) for t in (6, 7)]
+        pairs = [psum.tile([P, 2, M], F32, name=f"acc{s}", offset=4 * BANK * s) for s in range(3)]
+        late = [psum.tile([P, 1, M], F32, name=f"late{c}", offset=4 * BANK * (3 + c)) for c in range(2)]
         for h in range(2):
-            for t in range(4):
-                one_pass(early[t][:, 0, :], codes[t // 2], t, h)
-        for t in range(4, 8):
+            for t in range(2):
+                one_pass(pairs[0][:, t, :], codes[0], t, h, (h, t) == (0, 0), (h, t) == (1, 1))
+        finish(0, pairs[0:1])
+        codes.append(reused.tile([P, 2, BLOCK], U16, name="codes3", align_bytes=64, offset=2 * HALF_W + 4 * BLOCK))
+        for c in range(2):
+            part_half(codes[3], words[3], c)
+        for t in range(2, 8):
             for h in range(2):
-                one_pass(pair[:, t - 4, :] if t < 6 else late[t - 6][:, 0, :], codes[t // 2], t, h)
-        finish(0, early[0:2])
-        finish(2, early[2:4])
-        finish(4, [pair])
+                one_pass(pairs[t // 2][:, t % 2, :] if t < 6 else late[t - 6][:, 0, :], codes[t // 2], t, h, h == 0, h == 1)
+        finish(2, pairs[1:2])
+        finish(4, pairs[2:3])
         finish(6, late[0:1])
         finish(7, late[1:2])

@@ -38,6 +38,8 @@ def tile_list_tab4_tm_silu_kernel(tc, tab, w, b, offs, out):
         w_codes = [held.tile([P, M], U32, name=f"w_codes{h}", align_bytes=64) for h in range(2)]
         w_scales = [held.tile([P, M], U8, name=f"w_scales{h}", align_bytes=64) for h in range(2)]
         b_col = held.tile([P, 1], F32, name="b_col")
+        b_line = held.tile([1, M], F32, name="b_line")
+        b_square = held.tile([P, M], F32, name="b_square", align_bytes=64)
         b_row = held.tile([P, M], F32, name="b_row", align_bytes=64)
         ident = held.tile([P, P], F32, name="ident", align_bytes=64)
         warm = held.tile([P, 1], F32, name="warm")
@@ -80,13 +82,13 @@ def tile_list_tab4_tm_silu_kernel(tc, tab, w, b, offs, out):
             nc.scalar.activation(o[:], y[:], SILU)
             queue.dma_start(out[t0 * P : (t0 + n) * P, :].rearrange("(c p) n -> p c n", p=P), o[:])
 
+        nc.scalar.dma_start(b_line[:], b.rearrange("(o n) -> o n", o=1))
         scale_rows = tab[0, WORD_BYTES : WORD_BYTES + 32 * T].rearrange("(q t) -> q t", t=T)
         nc.sync.dma_start(scale_tab[0:32, :].bitcast(I32), scale_rows.bitcast(I32))
         nc.sync.dma_start(offsets[:], offs)
         load_w(0)
         nc.sync.dma_start(word_tab[:], tab[0, 0:WORD_BYTES].rearrange("(p x) -> p x", p=P).bitcast(I32))
         load_w(1)
-        nc.gpsimd.dma_start(b_col[:], b.rearrange("(p o) -> p o", o=1))
         nc.vector.memset(scale_tab[32:64, :].bitcast(I32), 0)
         nc.vector.memset(scale_tab[64:128, :].bitcast(I32), 0)
         nc.vector.memset(warm[:], 0.0)
@@ -94,8 +96,12 @@ def tile_list_tab4_tm_silu_kernel(tc, tab, w, b, offs, out):
 
         make_identity(nc, ident[:])
         b_bank = psum.tile([P, 7 * BANK], F32, name="b_bank", offset=0)
-        nc.tensor.transpose(b_bank[:, 0:M], b_col[:].to_broadcast([P, M]), ident[:])
-        nc.scalar.copy(b_row[:], b_bank[:, 0:M])
+        nc.gpsimd.memset(b_square[:], 0.0)
+        nc.scalar.copy(b_square[0:1, :], b_line[:])
+        nc.tensor.transpose(b_bank[:, 0:P], b_square[:], ident[:])
+        nc.scalar.copy(b_col[:], b_bank[:, 0:1])
+        nc.tensor.transpose(b_bank[:, BANK : BANK + M], b_col[:].to_broadcast([P, M]), ident[:])
+        nc.scalar.copy(b_row[:], b_bank[:, BANK : BANK + M])
 
         interleave(0)
         planes = [reused.tile([P, S], U8, name=f"plane{h}", align_bytes=64, offset=h * S) for h in range(2)]

@@ -49,7 +49,7 @@ def tile_list_tab4_tm_silu_kernel(tc, tab, w, b, offs, out):
             nc.sync.dma_start(w_raw[h][:].rearrange("p i n -> p (i n)"), w[512 * h : 512 * (h + 1), :].rearrange("(p i) n -> p (i n)", i=4))
 
         def interleave(h):
-            nc.scalar.activation(w_grp[h][:], w_raw[h][:].rearrange("p i n -> p n i"), COPY)
+            nc.scalar.activation(w_grp[h][:].rearrange("p (c j) i -> p c i j", j=4), w_raw[h][:].rearrange("p i (c j) -> p c i j", j=4), COPY)
 
         def quantize(h):
             nc.vector.quantize_mx(out=w_codes[h][:].bitcast(FP8X4), scales=w_scales[h][:], in_=w_grp[h][:].rearrange("p n i -> p (n i)"))
@@ -109,7 +109,7 @@ def tile_list_tab4_tm_silu_kernel(tc, tab, w, b, offs, out):
         quantize(0)
         nc.vector.tensor_copy(planes[0][0:4, :].bitcast(I32), picked[0:4, :].bitcast(I32))
         for h, q in [(h, q) for h in range(2) for q in range(4)][1:]:
-            queue = nc.scalar if q == 1 or (h, q) == (0, 3) else nc.sync
+            queue = nc.scalar if h == 1 and q < 3 else nc.sync
             queue.dma_start(planes[h][32 * q : 32 * q + 4, :].bitcast(I32), picked[16 * h + 4 * q : 16 * h + 4 * q + 4, :].bitcast(I32))
 
         interleave(1)

@@ -18,130 +18,141 @@ ADD = mybir.AluOpType.add
 
 P = 128
 WORD_BYTES = 512 * T
-BLOCK = 256
-HALF_W = 4 * M * 4
-BANK = 512
+CHUNK = 256
+KIB = 1024
+BANK = 2048
+FIRST, SECOND = 0, 1
+HALF = 3 * S // 4
 
 
 def tile_list_tab4_tm_silu_kernel(tc, tab, w, b, offs, out):
     nc = tc.nc
     with (
         tc.tile_pool(name="held", bufs=1) as held,
-        tc.tile_pool(name="reused", bufs=1) as reused,
+        tc.tile_pool(name="laid", bufs=1) as laid,
         tc.psum_pool(name="psum", bufs=1) as psum,
     ):
+        def at(name, shape, dtype, kib):
+            return laid.tile(shape, dtype, name=name, align_bytes=64, offset=kib * KIB)
+
         offsets = held.tile([P, S // 16], U16, name="offsets")
         scale_tab = held.tile([P, T], U8, name="scale_tab", align_bytes=64)
         word_tab = held.tile([P, T], I32, name="word_tab", align_bytes=64)
-        w_raw = [reused.tile([P, 4, M], F32, name=f"w_raw{h}", align_bytes=64, offset=h * HALF_W) for h in range(2)]
+        picked = held.tile([P, S], U8, name="picked", align_bytes=64)
+        w_raw = {FIRST: at("w_raw_first", [P, 4, M], F32, 0), SECOND: at("w_raw_second", [P, 4, M], F32, 2)}
         w_grp = [held.tile([P, M, 4], BF16, name=f"w_grp{h}", align_bytes=64) for h in range(2)]
         w_codes = [held.tile([P, M], U32, name=f"w_codes{h}", align_bytes=64) for h in range(2)]
         w_scales = [held.tile([P, M], U8, name=f"w_scales{h}", align_bytes=64) for h in range(2)]
-        b_col = held.tile([P, 1], F32, name="b_col")
         b_line = held.tile([1, M], F32, name="b_line")
         b_square = held.tile([P, M], F32, name="b_square", align_bytes=64)
+        b_col = held.tile([P, 1], F32, name="b_col")
         b_row = held.tile([P, M], F32, name="b_row", align_bytes=64)
         ident = held.tile([P, P], F32, name="ident", align_bytes=64)
         warm = held.tile([P, 1], F32, name="warm")
-        picked = held.tile([P, S], U8, name="picked", align_bytes=64)
-
-        def load_w(h):
-            nc.sync.dma_start(w_raw[h][:].rearrange("p i n -> p (i n)"), w[512 * h : 512 * (h + 1), :].rearrange("(p i) n -> p (i n)", i=4))
-
-        def interleave(h):
-            nc.scalar.activation(w_grp[h][:].rearrange("p (c j) i -> p c i j", j=4), w_raw[h][:].rearrange("p i (c j) -> p c i j", j=4), COPY)
-
-        def quantize(h):
-            nc.vector.quantize_mx(out=w_codes[h][:].bitcast(FP8X4), scales=w_scales[h][:], in_=w_grp[h][:].rearrange("p n i -> p (n i)"))
-
-        def gather(g, s):
-            t0 = s * BLOCK
-            nc.vector.tensor_copy(g[:], word_tab[:].bitcast(U32).indirect(offsets[:, t0 // 16 : (t0 + BLOCK) // 16]))
-
-        def part(cd, g):
-            nc.vector.tensor_copy(cd[:], g[:].bitcast(U16).rearrange("p (t h) -> p h t", h=2))
-
-        def part_half(cd, g, c):
-            nc.vector.tensor_copy(cd[:, :, c * P : (c + 1) * P], g[:, c * P : (c + 1) * P].bitcast(U16).rearrange("p (t h) -> p h t", h=2))
-
-        def one_pass(acc, cd, t, h, start, stop):
-            raw = cd[:].rearrange("p h t -> p (h t)").bitcast(U8)
-            b0 = 2 * (h * BLOCK + (t % 2) * P)
-            nc.tensor.matmul_mx(out=acc, lhsT=raw[:, b0 : b0 + 2 * P].bitcast(FP4X4), lhsT_scale=planes[h][:, t * P : (t + 1) * P],
-                                rhs=w_codes[h][:].bitcast(FP8X4), rhs_scale=w_scales[h][:], start=start, stop=stop)
-
-        def finish(t0, accs, queue=nc.sync):
-            n = sum(acc.shape[1] for acc in accs)
-            y = held.tile([P, n, M], F32, name=f"y{t0}", align_bytes=64)
-            o = held.tile([P, n, M], F32, name=f"o{t0}", align_bytes=64)
-            c = 0
-            for acc in accs:
-                k = acc.shape[1]
-                nc.vector.tensor_tensor(y[:, c : c + k, :], acc[:], b_row[:].unsqueeze(1).to_broadcast([P, k, M]), ADD)
-                c = c + k
-            nc.scalar.activation(o[:], y[:], SILU)
-            queue.dma_start(out[t0 * P : (t0 + n) * P, :].rearrange("(c p) n -> p c n", p=P), o[:])
 
         nc.scalar.dma_start(b_line[:], b.rearrange("(o n) -> o n", o=1))
         scale_rows = tab[0, WORD_BYTES : WORD_BYTES + 32 * T].rearrange("(q t) -> q t", t=T)
         nc.sync.dma_start(scale_tab[0:32, :].bitcast(I32), scale_rows.bitcast(I32))
         nc.sync.dma_start(offsets[:], offs)
-        load_w(0)
+        def load_w(h):
+            nc.sync.dma_start(w_raw[h][:].rearrange("p i n -> p (i n)"), w[512 * h : 512 * (h + 1), :].rearrange("(p i) n -> p (i n)", i=4))
+
+        load_w(FIRST)
         nc.sync.dma_start(word_tab[:], tab[0, 0:WORD_BYTES].rearrange("(p x) -> p x", p=P).bitcast(I32))
-        load_w(1)
+        load_w(SECOND)
         nc.vector.memset(scale_tab[32:64, :].bitcast(I32), 0)
         nc.vector.memset(scale_tab[64:128, :].bitcast(I32), 0)
         nc.vector.memset(warm[:], 0.0)
         nc.scalar.activation(warm[:], warm[:], SILU)
 
         make_identity(nc, ident[:])
-        b_bank = psum.tile([P, 7 * BANK], F32, name="b_bank", offset=0)
+        b_banks = psum.tile([P, 5, BANK // 4], F32, name="b_banks", offset=0)
         nc.gpsimd.memset(b_square[:], 0.0)
         nc.scalar.copy(b_square[0:1, :], b_line[:])
-        nc.tensor.transpose(b_bank[:, 0:P], b_square[:], ident[:])
-        nc.scalar.copy(b_col[:], b_bank[:, 0:1])
-        nc.tensor.transpose(b_bank[:, BANK : BANK + M], b_col[:].to_broadcast([P, M]), ident[:])
-        nc.scalar.copy(b_row[:], b_bank[:, BANK : BANK + M])
+        nc.tensor.transpose(b_banks[:, 0, 0:P], b_square[:], ident[:])
+        nc.scalar.copy(b_col[:], b_banks[:, 0, 0:1])
+        nc.tensor.transpose(b_banks[:, 1, 0:M], b_col[:].to_broadcast([P, M]), ident[:])
+        nc.scalar.copy(b_row[:], b_banks[:, 1, 0:M])
 
-        interleave(0)
-        planes = [reused.tile([P, S], U8, name=f"plane{h}", align_bytes=64, offset=h * S) for h in range(2)]
-        nc.vector.tensor_copy(picked[:], scale_tab[:].indirect(offsets[:]))
-        quantize(0)
-        nc.vector.tensor_copy(planes[0][0:4, :].bitcast(I32), picked[0:4, :].bitcast(I32))
-        for h, q in [(h, q) for h in range(2) for q in range(4)][1:]:
-            queue = nc.scalar if h == 1 and q < 3 else nc.sync
-            queue.dma_start(planes[h][32 * q : 32 * q + 4, :].bitcast(I32), picked[16 * h + 4 * q : 16 * h + 4 * q + 4, :].bitcast(I32))
+        def round_w(h):
+            nc.scalar.activation(w_grp[h][:].rearrange("p (c j) i -> p c i j", j=4), w_raw[h][:].rearrange("p i (c j) -> p c i j", j=4), COPY)
 
-        interleave(1)
+        def quantize(h):
+            nc.vector.quantize_mx(out=w_codes[h][:].bitcast(FP8X4), scales=w_scales[h][:], in_=w_grp[h][:].rearrange("p n i -> p (n i)"))
 
-        words = [held.tile([P, BLOCK], U32, name="words0", align_bytes=64), reused.tile([P, BLOCK], U32, name="words1", align_bytes=64, offset=2 * HALF_W)]
-        codes = [reused.tile([P, 2, BLOCK], U16, name="codes0", align_bytes=64, offset=2 * HALF_W + 4 * BLOCK)]
-        for s in range(2):
-            gather(words[s], s)
-        part(codes[0], words[0])
-        quantize(1)
-        words.append(reused.tile([P, BLOCK], U32, name="words2", align_bytes=64, offset=HALF_W))
-        gather(words[2], 2)
-        codes.append(reused.tile([P, 2, BLOCK], U16, name="codes1", align_bytes=64, offset=HALF_W + 4 * BLOCK))
-        part(codes[1], words[1])
-        codes.append(held.tile([P, 2, BLOCK], U16, name="codes2", align_bytes=64))
-        part(codes[2], words[2])
-        words.append(reused.tile([P, BLOCK], U32, name="words3", align_bytes=64, offset=2 * HALF_W))
-        gather(words[3], 3)
+        def gather(words, s):
+            nc.vector.tensor_copy(words[:], word_tab[:].bitcast(U32).indirect(offsets[:, s * CHUNK // 16 : (s + 1) * CHUNK // 16]))
 
-        pairs = [psum.tile([P, 2, M], F32, name=f"acc{s}", offset=4 * BANK * s) for s in range(3)]
-        late = [psum.tile([P, 1, M], F32, name=f"late{c}", offset=4 * BANK * (3 + c)) for c in range(2)]
-        for h in range(2):
+        def part(codes, words, c0, c1):
+            nc.vector.tensor_copy(codes[:, :, c0:c1], words[:, c0:c1].bitcast(U16).rearrange("p (t h) -> p h t", h=2))
+
+        def one_pass(acc, codes, t, h, start, stop):
+            raw = codes[:].rearrange("p h t -> p (h t)").bitcast(U8)
+            b0 = 2 * (h * CHUNK + (t % 2) * P)
+            nc.tensor.matmul_mx(out=acc, lhsT=raw[:, b0 : b0 + 2 * P].bitcast(FP4X4), lhsT_scale=planes[h][:, t * P : (t + 1) * P],
+                                rhs=w_codes[h][:].bitcast(FP8X4), rhs_scale=w_scales[h][:], start=start, stop=stop)
+
+        def finish(t0, acc):
+            n = acc.shape[1]
+            y = held.tile([P, n, M], F32, name=f"y{t0}", align_bytes=64)
+            o = held.tile([P, n, M], F32, name=f"o{t0}", align_bytes=64)
+            nc.vector.tensor_tensor(y[:], acc[:], b_row[:].unsqueeze(1).to_broadcast([P, n, M]), ADD)
+            nc.scalar.activation(o[:], y[:], SILU)
+            nc.sync.dma_start(out[t0 * P : (t0 + n) * P, :].rearrange("(c p) n -> p c n", p=P), o[:])
+
+        def pick(c0, c1):
+            nc.vector.tensor_copy(picked[:, c0:c1], scale_tab[:].indirect(offsets[:, c0 // 16 : c1 // 16]))
+
+        def move(queue, h, q, c0, c1):
+            queue.dma_start(planes[h][32 * q : 32 * q + 4, c0:c1].bitcast(I32), picked[16 * h + 4 * q : 16 * h + 4 * q + 4, c0:c1].bitcast(I32))
+
+        def keep(c0, c1):
+            nc.vector.tensor_copy(planes[0][0:4, c0:c1].bitcast(I32), picked[0:4, c0:c1].bitcast(I32))
+
+        round_w(FIRST)
+        planes = [at(f"plane{h}", [P, S], U8, h) for h in range(2)]
+        pick(0, HALF)
+        for q in range(1, 4):
+            move(nc.sync, FIRST, q, 0, HALF)
+        pick(HALF, S)
+        keep(0, HALF)
+        quantize(FIRST)
+        keep(HALF, S)
+        for q in range(4):
+            move(nc.scalar if q < 2 else nc.sync, SECOND, q, 0, S)
+        for q in range(1, 4):
+            move(nc.sync, FIRST, q, HALF, S)
+        round_w(SECOND)
+        words0 = held.tile([P, CHUNK], U32, name="words0", align_bytes=64)
+        words1 = at("words1", [P, CHUNK], U32, 4)
+        codes0 = at("codes0", [P, 2, CHUNK], U16, 5)
+        gather(words0, 0)
+        gather(words1, 1)
+        part(codes0, words0, 0, CHUNK)
+        quantize(SECOND)
+        words2 = at("words2", [P, CHUNK], U32, 2)
+        gather(words2, 2)
+        codes1 = at("codes1", [P, 2, CHUNK], U16, 3)
+        part(codes1, words1, 0, CHUNK)
+        codes2 = held.tile([P, 2, CHUNK], U16, name="codes2", align_bytes=64)
+        part(codes2, words2, 0, CHUNK)
+        words3 = at("words3", [P, CHUNK], U32, 4)
+        gather(words3, 3)
+
+        pairs = [psum.tile([P, 2, M], F32, name=f"pair{s}", offset=BANK * s) for s in range(3)]
+        late = [psum.tile([P, 1, M], F32, name=f"late{c}", offset=BANK * (3 + c)) for c in range(2)]
+        for h in (FIRST, SECOND):
             for t in range(2):
-                one_pass(pairs[0][:, t, :], codes[0], t, h, (h, t) == (0, 0), (h, t) == (1, 1))
-        finish(0, pairs[0:1])
-        codes.append(reused.tile([P, 2, BLOCK], U16, name="codes3", align_bytes=64, offset=2 * HALF_W + 4 * BLOCK))
+                one_pass(pairs[0][:, t, :], codes0, t, h, (h, t) == (FIRST, 0), (h, t) == (SECOND, 1))
+        finish(0, pairs[0])
+        codes3 = at("codes3", [P, 2, CHUNK], U16, 5)
         for c in range(2):
-            part_half(codes[3], words[3], c)
+            part(codes3, words3, c * P, (c + 1) * P)
+        codes = [codes0, codes1, codes2, codes3]
         for t in range(2, 8):
-            for h in range(2):
-                one_pass(pairs[t // 2][:, t % 2, :] if t < 6 else late[t - 6][:, 0, :], codes[t // 2], t, h, h == 0, h == 1)
-        finish(2, pairs[1:2])
-        finish(4, pairs[2:3])
-        finish(6, late[0:1])
-        finish(7, late[1:2])
+            for h in (FIRST, SECOND):
+                one_pass(pairs[t // 2][:, t % 2, :] if t < 6 else late[t - 6][:, 0, :], codes[t // 2], t, h, h == FIRST, h == SECOND)
+        finish(2, pairs[1])
+        finish(4, pairs[2])
+        finish(6, late[0])
+        finish(7, late[1])

@@ -117,10 +117,9 @@ def tile_list_tab4_tm_silu_kernel(tc, tab, w, b, offs, out):
         pick(HALF, S)
         keep(0, HALF)
         quantize(FIRST)
-        keep(HALF, S)
         for q in range(4):
             move(nc.scalar if q < 2 else nc.sync, SECOND, q, 0, S)
-        for q in range(1, 4):
+        for q in range(4):
             move(nc.sync, FIRST, q, HALF, S)
         round_w(SECOND)
         words0 = held.tile([P, CHUNK], U32, name="words0", align_bytes=64)
@@ -128,12 +127,14 @@ def tile_list_tab4_tm_silu_kernel(tc, tab, w, b, offs, out):
         codes0 = at("codes0", [P, 2, CHUNK], U16, 5)
         gather(words0, 0)
         gather(words1, 1)
-        part(codes0, words0, 0, CHUNK)
+        for c in range(2):
+            part(codes0, words0, c * P, (c + 1) * P)
         quantize(SECOND)
         words2 = at("words2", [P, CHUNK], U32, 2)
         gather(words2, 2)
         codes1 = at("codes1", [P, 2, CHUNK], U16, 3)
-        part(codes1, words1, 0, CHUNK)
+        for c in range(2):
+            part(codes1, words1, c * P, (c + 1) * P)
         codes2 = held.tile([P, 2, CHUNK], U16, name="codes2", align_bytes=64)
         part(codes2, words2, 0, CHUNK)
         words3 = at("words3", [P, CHUNK], U32, 4)

@@ -21,7 +21,7 @@ WORD_BYTES = 512 * T
 CHUNK = 256
 KIB = 1024
 BANK = 2048
-FIRST, SECOND = 0, 1
+FIRST, SECOND = 1, 0
 HALF = 3 * S // 4
 
 
@@ -112,15 +112,16 @@ def tile_list_tab4_tm_silu_kernel(tc, tab, w, b, offs, out):
         round_w(FIRST)
         planes = [at(f"plane{h}", [P, S], U8, h) for h in range(2)]
         pick(0, HALF)
-        for q in range(1, 4):
-            move(nc.sync, FIRST, q, 0, HALF)
+        for q in range(4):
+            move(nc.scalar if q % 2 else nc.sync, FIRST, q, 0, HALF)
         pick(HALF, S)
         keep(0, HALF)
         quantize(FIRST)
-        for q in range(4):
-            move(nc.scalar if q < 2 else nc.sync, SECOND, q, 0, S)
+        for q in range(1, 4):
+            move(nc.sync, SECOND, q, 0, S)
         for q in range(4):
             move(nc.sync, FIRST, q, HALF, S)
+        move(nc.sync, SECOND, 0, HALF, S)
         round_w(SECOND)
         words0 = held.tile([P, CHUNK], U32, name="words0", align_bytes=64)
         words1 = at("words1", [P, CHUNK], U32, 4)

@@ -57,8 +57,8 @@ def tile_list_tab4_tm_silu_kernel(tc, tab, w, b, offs, out):
         def load_w(h):
             nc.sync.dma_start(w_raw[h][:].rearrange("p i n -> p (i n)"), w[512 * h : 512 * (h + 1), :].rearrange("(p i) n -> p (i n)", i=4))
 
-        load_w(FIRST)
         nc.sync.dma_start(word_tab[:], tab[0, 0:WORD_BYTES].rearrange("(p x) -> p x", p=P).bitcast(I32))
+        load_w(FIRST)
         load_w(SECOND)
         nc.vector.memset(scale_tab[32:64, :].bitcast(I32), 0)
         nc.vector.memset(scale_tab[64:128, :].bitcast(I32), 0)
@@ -110,13 +110,12 @@ def tile_list_tab4_tm_silu_kernel(tc, tab, w, b, offs, out):
             nc.vector.tensor_copy(planes[0][0:4, c0:c1].bitcast(I32), picked[0:4, c0:c1].bitcast(I32))
 
         round_w(FIRST)
-        planes = [at(f"plane{h}", [P, S], U8, h) for h in range(2)]
+        planes = [held.tile([P, S], U8, name=f"plane{h}", align_bytes=64) for h in range(2)]
         pick(0, HALF)
         for q in range(4):
             move(nc.scalar if q % 2 else nc.sync, FIRST, q, 0, HALF)
         pick(HALF, S)
         keep(0, HALF)
-        quantize(FIRST)
         for q in range(1, 4):
             move(nc.sync, SECOND, q, 0, S)
         for q in range(4):
@@ -130,6 +129,7 @@ def tile_list_tab4_tm_silu_kernel(tc, tab, w, b, offs, out):
         gather(words1, 1)
         for c in range(2):
             part(codes0, words0, c * P, (c + 1) * P)
+        quantize(FIRST)
         quantize(SECOND)
         words2 = at("words2", [P, CHUNK], U32, 2)
         gather(words2, 2)

@@ -22,7 +22,7 @@ CHUNK = 256
 KIB = 1024
 BANK = 2048
 FIRST, SECOND = 1, 0
-HALF = 3 * S // 4
+HALF = S // 2
 
 
 def tile_list_tab4_tm_silu_kernel(tc, tab, w, b, offs, out):
@@ -38,14 +38,13 @@ def tile_list_tab4_tm_silu_kernel(tc, tab, w, b, offs, out):
         offsets = held.tile([P, S // 16], U16, name="offsets")
         scale_tab = held.tile([P, T], U8, name="scale_tab", align_bytes=64)
         word_tab = held.tile([P, T], I32, name="word_tab", align_bytes=64)
-        picked = held.tile([P, S], U8, name="picked", align_bytes=64)
+        picked = at("picked", [P, S], U8, 5)
         w_raw = {FIRST: at("w_raw_first", [P, 4, M], F32, 0), SECOND: at("w_raw_second", [P, 4, M], F32, 2)}
-        w_grp = [held.tile([P, M, 4], BF16, name=f"w_grp{h}", align_bytes=64) for h in range(2)]
         w_codes = [held.tile([P, M], U32, name=f"w_codes{h}", align_bytes=64) for h in range(2)]
         w_scales = [held.tile([P, M], U8, name=f"w_scales{h}", align_bytes=64) for h in range(2)]
         b_line = held.tile([1, M], F32, name="b_line")
         b_square = held.tile([P, M], F32, name="b_square", align_bytes=64)
-        b_col = held.tile([P, 1], F32, name="b_col")
+        b_col = laid.tile([P, 2, 16], F32, name="b_col", align_bytes=64, offset=8 * KIB - 64)
         b_row = held.tile([P, M], F32, name="b_row", align_bytes=64)
         ident = held.tile([P, P], F32, name="ident", align_bytes=64)
         warm = held.tile([P, 1], F32, name="warm")
@@ -66,13 +65,16 @@ def tile_list_tab4_tm_silu_kernel(tc, tab, w, b, offs, out):
         nc.scalar.activation(warm[:], warm[:], SILU)
 
         make_identity(nc, ident[:])
-        b_banks = psum.tile([P, 5, BANK // 4], F32, name="b_banks", offset=0)
+        b_banks = psum.tile([P, 6, BANK // 4], F32, name="b_banks", offset=0)
         nc.gpsimd.memset(b_square[:], 0.0)
         nc.scalar.copy(b_square[0:1, :], b_line[:])
         nc.tensor.transpose(b_banks[:, 0, 0:P], b_square[:], ident[:])
-        nc.scalar.copy(b_col[:], b_banks[:, 0, 0:1])
-        nc.tensor.transpose(b_banks[:, 1, 0:M], b_col[:].to_broadcast([P, M]), ident[:])
-        nc.scalar.copy(b_row[:], b_banks[:, 1, 0:M])
+        nc.scalar.copy(b_col[:, 0, 0:1], b_banks[:, 0, 0:1])
+        b_spread = psum.tile([P, M], F32, name="b_spread", offset=7 * BANK)
+        nc.tensor.transpose(b_spread[:], b_col[:, 0, 0:1].to_broadcast([P, M]), ident[:])
+        nc.scalar.copy(b_row[:], b_spread[:])
+
+        w_grp = {FIRST: at("w_grp_first", [P, M, 4], BF16, 7), SECOND: at("w_grp_second", [P, M, 4], BF16, 8)}
 
         def round_w(h):
             nc.scalar.activation(w_grp[h][:].rearrange("p (c j) i -> p c i j", j=4), w_raw[h][:].rearrange("p i (c j) -> p c i j", j=4), COPY)
@@ -80,23 +82,24 @@ def tile_list_tab4_tm_silu_kernel(tc, tab, w, b, offs, out):
         def quantize(h):
             nc.vector.quantize_mx(out=w_codes[h][:].bitcast(FP8X4), scales=w_scales[h][:], in_=w_grp[h][:].rearrange("p n i -> p (n i)"))
 
-        def gather(words, s):
-            nc.vector.tensor_copy(words[:], word_tab[:].bitcast(U32).indirect(offsets[:, s * CHUNK // 16 : (s + 1) * CHUNK // 16]))
+        def gather(words, t0):
+            n = words.shape[1]
+            nc.vector.tensor_copy(words[:], word_tab[:].bitcast(U32).indirect(offsets[:, t0 * P // 16 : (t0 * P + n) // 16]))
 
-        def part(codes, words, c0, c1):
-            nc.vector.tensor_copy(codes[:, :, c0:c1], words[:, c0:c1].bitcast(U16).rearrange("p (t h) -> p h t", h=2))
+        def part(codes, words):
+            nc.vector.tensor_copy(codes[:], words[:].bitcast(U16).rearrange("p (t h) -> p h t", h=2))
 
-        def one_pass(acc, codes, t, h, start, stop):
+        def one_pass(acc, codes, c, t, h, start, stop):
             raw = codes[:].rearrange("p h t -> p (h t)").bitcast(U8)
-            b0 = 2 * (h * CHUNK + (t % 2) * P)
+            b0 = 2 * (h * codes.shape[2] + c * P)
             nc.tensor.matmul_mx(out=acc, lhsT=raw[:, b0 : b0 + 2 * P].bitcast(FP4X4), lhsT_scale=planes[h][:, t * P : (t + 1) * P],
                                 rhs=w_codes[h][:].bitcast(FP8X4), rhs_scale=w_scales[h][:], start=start, stop=stop)
 
-        def finish(t0, acc):
+        def finish(t0, acc, y=None):
             n = acc.shape[1]
-            y = held.tile([P, n, M], F32, name=f"y{t0}", align_bytes=64)
+            y = y if y is not None else held.tile([P, n, M], F32, name=f"y{t0}", align_bytes=64)
             o = held.tile([P, n, M], F32, name=f"o{t0}", align_bytes=64)
-            nc.vector.tensor_tensor(y[:], acc[:], b_row[:].unsqueeze(1).to_broadcast([P, n, M]), ADD)
+            nc.vector.tensor_tensor(y[:], acc, b_row[:].unsqueeze(1).to_broadcast([P, n, M]), ADD)
             nc.scalar.activation(o[:], y[:], SILU)
             nc.sync.dma_start(out[t0 * P : (t0 + n) * P, :].rearrange("(c p) n -> p c n", p=P), o[:])
 
@@ -106,55 +109,48 @@ def tile_list_tab4_tm_silu_kernel(tc, tab, w, b, offs, out):
         def move(queue, h, q, c0, c1):
             queue.dma_start(planes[h][32 * q : 32 * q + 4, c0:c1].bitcast(I32), picked[16 * h + 4 * q : 16 * h + 4 * q + 4, c0:c1].bitcast(I32))
 
-        def keep(c0, c1):
-            nc.vector.tensor_copy(planes[0][0:4, c0:c1].bitcast(I32), picked[0:4, c0:c1].bitcast(I32))
-
         round_w(FIRST)
         planes = [held.tile([P, S], U8, name=f"plane{h}", align_bytes=64) for h in range(2)]
         pick(0, HALF)
         for q in range(4):
-            move(nc.scalar if q % 2 else nc.sync, FIRST, q, 0, HALF)
+            move(nc.sync, FIRST, q, 0, HALF)
         pick(HALF, S)
-        keep(0, HALF)
-        for q in range(1, 4):
+        for q in range(4):
             move(nc.sync, SECOND, q, 0, S)
         for q in range(4):
             move(nc.sync, FIRST, q, HALF, S)
-        move(nc.sync, SECOND, 0, HALF, S)
         round_w(SECOND)
-        words0 = held.tile([P, CHUNK], U32, name="words0", align_bytes=64)
-        words1 = at("words1", [P, CHUNK], U32, 4)
-        codes0 = at("codes0", [P, 2, CHUNK], U16, 5)
-        gather(words0, 0)
-        gather(words1, 1)
-        for c in range(2):
-            part(codes0, words0, c * P, (c + 1) * P)
-        quantize(FIRST)
-        quantize(SECOND)
-        words2 = at("words2", [P, CHUNK], U32, 2)
-        gather(words2, 2)
-        codes1 = at("codes1", [P, 2, CHUNK], U16, 3)
-        for c in range(2):
-            part(codes1, words1, c * P, (c + 1) * P)
-        codes2 = held.tile([P, 2, CHUNK], U16, name="codes2", align_bytes=64)
-        part(codes2, words2, 0, CHUNK)
-        words3 = at("words3", [P, CHUNK], U32, 4)
-        gather(words3, 3)
 
-        pairs = [psum.tile([P, 2, M], F32, name=f"pair{s}", offset=BANK * s) for s in range(3)]
-        late = [psum.tile([P, 1, M], F32, name=f"late{c}", offset=BANK * (3 + c)) for c in range(2)]
+        words = [held.tile([P, CHUNK], U32, name=f"words{s}", align_bytes=64) for s in range(2)] + [at("words2", [P, CHUNK], U32, 1)]
+        codes = [held.tile([P, 2, CHUNK], U16, name="codes0", align_bytes=64), at("codes1", [P, 2, CHUNK], U16, 0), at("codes2", [P, 2, CHUNK], U16, 2)]
+        words6 = at("words6", [P, P], U32, 3)
+        words7 = laid.tile([P, P], U32, name="words7", align_bytes=64, offset=3 * KIB + 4 * P)
+        codes6 = held.tile([P, 2, P], U16, name="codes6", align_bytes=64)
+        gather(words[0], 0)
+        gather(words[1], 2)
+        part(codes[0], words[0])
+        quantize(FIRST)
+        gather(words[2], 4)
+        part(codes[1], words[1])
+        quantize(SECOND)
+        gather(words6, 6)
+        part(codes[2], words[2])
+        gather(words7, 7)
+        part(codes6, words6)
+
+        pairs = [psum.tile([P, 2, M], F32, name=f"pair{s}", offset=BANK * s) for s in range(2)]
+        late = [psum.tile([P, 1, M], F32, name=f"late{c}", offset=BANK * (2 + c)) for c in range(4)]
         for h in (FIRST, SECOND):
-            for t in range(2):
-                one_pass(pairs[0][:, t, :], codes0, t, h, (h, t) == (FIRST, 0), (h, t) == (SECOND, 1))
-        finish(0, pairs[0])
-        codes3 = at("codes3", [P, 2, CHUNK], U16, 5)
-        for c in range(2):
-            part(codes3, words3, c * P, (c + 1) * P)
-        codes = [codes0, codes1, codes2, codes3]
-        for t in range(2, 8):
-            for h in (FIRST, SECOND):
-                one_pass(pairs[t // 2][:, t % 2, :] if t < 6 else late[t - 6][:, 0, :], codes[t // 2], t, h, h == FIRST, h == SECOND)
-        finish(2, pairs[1])
-        finish(4, pairs[2])
-        finish(6, late[0])
-        finish(7, late[1])
+            for t in range(4):
+                one_pass(pairs[t // 2][:, t % 2, :], codes[t // 2], t % 2, t, h, (h, t % 2) == (FIRST, 0), (h, t % 2) == (SECOND, 1))
+        finish(0, pairs[0][:])
+        codes7 = at("codes7", [P, 2, P], U16, 5)
+        part(codes7, words7)
+        finish(2, pairs[1][:], laid.tile([P, 2, M], F32, name="y2", align_bytes=64, offset=5 * KIB + 4 * P))
+        for h in (FIRST, SECOND):
+            for c in range(3):
+                one_pass(late[c][:, 0, :], codes[2] if c < 2 else codes6, c % 2, 4 + c, h, h == FIRST, h == SECOND)
+        for h in (FIRST, SECOND):
+            one_pass(late[3][:, 0, :], codes7, 0, 7, h, h == FIRST, h == SECOND)
+        for c in range(4):
+            finish(4 + c, late[c][:])

@@ -21,8 +21,8 @@ WORD_BYTES = 512 * T
 CHUNK = 256
 KIB = 1024
 BANK = 2048
-FIRST, SECOND = 1, 0
-HALF = S // 2
+FIRST, SECOND = 0, 1
+HALF = 3 * S // 4
 
 
 def tile_list_tab4_tm_silu_kernel(tc, tab, w, b, offs, out):
@@ -38,8 +38,8 @@ def tile_list_tab4_tm_silu_kernel(tc, tab, w, b, offs, out):
         offsets = held.tile([P, S // 16], U16, name="offsets")
         scale_tab = held.tile([P, T], U8, name="scale_tab", align_bytes=64)
         word_tab = held.tile([P, T], I32, name="word_tab", align_bytes=64)
-        picked = at("picked", [P, S], U8, 5)
-        w_raw = {FIRST: at("w_raw_first", [P, 4, M], F32, 0), SECOND: at("w_raw_second", [P, 4, M], F32, 2)}
+        picked = held.tile([P, S], U8, name="picked", align_bytes=64)
+        w_raw = {FIRST: at("w_raw_first", [P, 4, M], F32, 0), SECOND: at("w_raw_second", [P, 4, M], F32, 3)}
         w_codes = [held.tile([P, M], U32, name=f"w_codes{h}", align_bytes=64) for h in range(2)]
         w_scales = [held.tile([P, M], U8, name=f"w_scales{h}", align_bytes=64) for h in range(2)]
         b_line = held.tile([1, M], F32, name="b_line")
@@ -65,7 +65,7 @@ def tile_list_tab4_tm_silu_kernel(tc, tab, w, b, offs, out):
         nc.scalar.activation(warm[:], warm[:], SILU)
 
         make_identity(nc, ident[:])
-        b_banks = psum.tile([P, 6, BANK // 4], F32, name="b_banks", offset=0)
+        b_banks = psum.tile([P, 7, BANK // 4], F32, name="b_banks", offset=0)
         nc.gpsimd.memset(b_square[:], 0.0)
         nc.scalar.copy(b_square[0:1, :], b_line[:])
         nc.tensor.transpose(b_banks[:, 0, 0:P], b_square[:], ident[:])
@@ -92,65 +92,88 @@ def tile_list_tab4_tm_silu_kernel(tc, tab, w, b, offs, out):
         def one_pass(acc, codes, c, t, h, start, stop):
             raw = codes[:].rearrange("p h t -> p (h t)").bitcast(U8)
             b0 = 2 * (h * codes.shape[2] + c * P)
-            nc.tensor.matmul_mx(out=acc, lhsT=raw[:, b0 : b0 + 2 * P].bitcast(FP4X4), lhsT_scale=planes[h][:, t * P : (t + 1) * P],
+            nc.tensor.matmul_mx(out=acc, lhsT=raw[:, b0 : b0 + 2 * P].bitcast(FP4X4), lhsT_scale=plane(h, t),
                                 rhs=w_codes[h][:].bitcast(FP8X4), rhs_scale=w_scales[h][:], start=start, stop=stop)
 
-        def finish(t0, acc, y=None):
+        def finish(t, acc):
             n = acc.shape[1]
-            y = y if y is not None else held.tile([P, n, M], F32, name=f"y{t0}", align_bytes=64)
-            o = held.tile([P, n, M], F32, name=f"o{t0}", align_bytes=64)
-            nc.vector.tensor_tensor(y[:], acc, b_row[:].unsqueeze(1).to_broadcast([P, n, M]), ADD)
-            nc.scalar.activation(o[:], y[:], SILU)
-            nc.sync.dma_start(out[t0 * P : (t0 + n) * P, :].rearrange("(c p) n -> p c n", p=P), o[:])
+            y = held.tile([P, n, M], F32, name=f"y{t}", align_bytes=64)[:]
+            nc.vector.tensor_tensor(y, acc, b_row[:].unsqueeze(1).to_broadcast([P, n, M]), ADD)
+            nc.scalar.activation(o[:, t : t + n, :], y, SILU)
+
+        def store(t0, n):
+            nc.sync.dma_start(out[t0 * P : (t0 + n) * P, :].rearrange("(c p) n -> p c n", p=P), o[:, t0 : t0 + n, :])
 
         def pick(c0, c1):
             nc.vector.tensor_copy(picked[:, c0:c1], scale_tab[:].indirect(offsets[:, c0 // 16 : c1 // 16]))
 
-        def move(queue, h, q, c0, c1):
-            queue.dma_start(planes[h][32 * q : 32 * q + 4, c0:c1].bitcast(I32), picked[16 * h + 4 * q : 16 * h + 4 * q + 4, c0:c1].bitcast(I32))
+        def rows(h, q, c0, c1):
+            return picked[16 * h + 4 * q : 16 * h + 4 * q + 4, c0:c1].bitcast(I32)
+
+        def live(plane, q):
+            return plane[32 * q : 32 * q + 4, :].bitcast(I32)
 
         round_w(FIRST)
-        planes = [held.tile([P, S], U8, name=f"plane{h}", align_bytes=64) for h in range(2)]
+        first_early = held.tile([P, HALF], U8, name="first_early", align_bytes=64)
+        second = held.tile([P, S], U8, name="second", align_bytes=64)
         pick(0, HALF)
-        for q in range(4):
-            move(nc.sync, FIRST, q, 0, HALF)
+        for q in range(1, 4):
+            nc.sync.dma_start(live(first_early, q), rows(FIRST, q, 0, HALF))
         pick(HALF, S)
+        nc.vector.tensor_copy(live(first_early, 0), rows(FIRST, 0, 0, HALF))
         for q in range(4):
-            move(nc.sync, SECOND, q, 0, S)
-        for q in range(4):
-            move(nc.sync, FIRST, q, HALF, S)
+            nc.sync.dma_start(live(second, q), rows(SECOND, q, 0, S))
+        first_late = at("first_late", [P, S - HALF], U8, 0)
+        for q in range(1, 4):
+            nc.sync.dma_start(live(first_late, q), rows(FIRST, q, HALF, S))
         round_w(SECOND)
 
-        words = [held.tile([P, CHUNK], U32, name=f"words{s}", align_bytes=64) for s in range(2)] + [at("words2", [P, CHUNK], U32, 1)]
-        codes = [held.tile([P, 2, CHUNK], U16, name="codes0", align_bytes=64), at("codes1", [P, 2, CHUNK], U16, 0), at("codes2", [P, 2, CHUNK], U16, 2)]
-        words6 = at("words6", [P, P], U32, 3)
-        words7 = laid.tile([P, P], U32, name="words7", align_bytes=64, offset=3 * KIB + 4 * P)
+        def plane(h, t):
+            if h == SECOND:
+                return second[:, t * P : (t + 1) * P]
+            return first_early[:, t * P : (t + 1) * P] if t * P < HALF else first_late[:, t * P - HALF : (t + 1) * P - HALF]
+
+        words = [held.tile([P, CHUNK], U32, name=f"words{s}", align_bytes=64) for s in range(2)]
+        words.append(laid.tile([P, CHUNK], U32, name="words2", align_bytes=64, offset=KIB + S - HALF))
+        codes = [at("codes0", [P, 2, CHUNK], U16, 5), laid.tile([P, 2, CHUNK], U16, name="codes1", align_bytes=64, offset=S - HALF), at("codes2", [P, 2, CHUNK], U16, 3)]
+        words6 = at("words6", [P, P], U32, 4)
+        words7 = laid.tile([P, P], U32, name="words7", align_bytes=64, offset=4 * KIB + 4 * P)
         codes6 = held.tile([P, 2, P], U16, name="codes6", align_bytes=64)
         gather(words[0], 0)
         gather(words[1], 2)
         part(codes[0], words[0])
         quantize(FIRST)
-        gather(words[2], 4)
         part(codes[1], words[1])
+        gather(words[2], 4)
+        nc.vector.tensor_copy(live(first_late, 0), rows(FIRST, 0, HALF, S))
         quantize(SECOND)
         gather(words6, 6)
         part(codes[2], words[2])
         gather(words7, 7)
         part(codes6, words6)
 
-        pairs = [psum.tile([P, 2, M], F32, name=f"pair{s}", offset=BANK * s) for s in range(2)]
-        late = [psum.tile([P, 1, M], F32, name=f"late{c}", offset=BANK * (2 + c)) for c in range(4)]
+        o = held.tile([P, S // P, M], F32, name="o", align_bytes=64)
+        early = [psum.tile([P, 1, M], F32, name=f"early{t}", offset=BANK * t) for t in range(4)]
+        pair = psum.tile([P, 2, M], F32, name="pair", offset=BANK * 4)
+        late = [psum.tile([P, 1, M], F32, name=f"late{c}", offset=BANK * (5 + c)) for c in range(2)]
         for h in (FIRST, SECOND):
             for t in range(4):
-                one_pass(pairs[t // 2][:, t % 2, :], codes[t // 2], t % 2, t, h, (h, t % 2) == (FIRST, 0), (h, t % 2) == (SECOND, 1))
-        finish(0, pairs[0][:])
+                one_pass(early[t][:, 0, :], codes[t // 2], t % 2, t, h, h == FIRST, h == SECOND)
+        for h in (SECOND, FIRST):
+            for c in range(2):
+                one_pass(pair[:, c, :], codes[2], c, 4 + c, h, (h, c) == (SECOND, 0), (h, c) == (FIRST, 1))
+        finish(0, early[0][:])
         codes7 = at("codes7", [P, 2, P], U16, 5)
         part(codes7, words7)
-        finish(2, pairs[1][:], laid.tile([P, 2, M], F32, name="y2", align_bytes=64, offset=5 * KIB + 4 * P))
-        for h in (FIRST, SECOND):
-            for c in range(3):
-                one_pass(late[c][:, 0, :], codes[2] if c < 2 else codes6, c % 2, 4 + c, h, h == FIRST, h == SECOND)
-        for h in (FIRST, SECOND):
-            one_pass(late[3][:, 0, :], codes7, 0, 7, h, h == FIRST, h == SECOND)
-        for c in range(4):
-            finish(4 + c, late[c][:])
+        for c, last_codes in enumerate((codes6, codes7)):
+            for h in (FIRST, SECOND):
+                one_pass(late[c][:, 0, :], last_codes, 0, 6 + c, h, h == FIRST, h == SECOND)
+        for t in range(1, 4):
+            finish(t, early[t][:])
+            if t % 2:
+                store(t - 1, 2)
+        finish(4, pair[:])
+        store(4, 2)
+        for c in range(2):
+            finish(6 + c, late[c][:])
+            store(6 + c, 1)

@@ -38,7 +38,7 @@ def tile_list_tab4_tm_silu_kernel(tc, tab, w, b, offs, out):
         offsets = held.tile([P, S // 16], U16, name="offsets")
         scale_tab = held.tile([P, T], U8, name="scale_tab", align_bytes=64)
         word_tab = held.tile([P, T], I32, name="word_tab", align_bytes=64)
-        picked = held.tile([P, S], U8, name="picked", align_bytes=64)
+        picked = at("picked", [P, S], U8, 10)
         w_raw = {FIRST: at("w_raw_first", [P, 4, M], F32, 0), SECOND: at("w_raw_second", [P, 4, M], F32, 3)}
         w_codes = [held.tile([P, M], U32, name=f"w_codes{h}", align_bytes=64) for h in range(2)]
         w_scales = [held.tile([P, M], U8, name=f"w_scales{h}", align_bytes=64) for h in range(2)]
@@ -95,9 +95,9 @@ def tile_list_tab4_tm_silu_kernel(tc, tab, w, b, offs, out):
             nc.tensor.matmul_mx(out=acc, lhsT=raw[:, b0 : b0 + 2 * P].bitcast(FP4X4), lhsT_scale=plane(h, t),
                                 rhs=w_codes[h][:].bitcast(FP8X4), rhs_scale=w_scales[h][:], start=start, stop=stop)
 
-        def finish(t, acc):
+        def finish(t, acc, y=None):
             n = acc.shape[1]
-            y = held.tile([P, n, M], F32, name=f"y{t}", align_bytes=64)[:]
+            y = y if y is not None else held.tile([P, n, M], F32, name=f"y{t}", align_bytes=64)[:]
             nc.vector.tensor_tensor(y, acc, b_row[:].unsqueeze(1).to_broadcast([P, n, M]), ADD)
             nc.scalar.activation(o[:, t : t + n, :], y, SILU)
 
@@ -163,16 +163,17 @@ def tile_list_tab4_tm_silu_kernel(tc, tab, w, b, offs, out):
             for c in range(2):
                 one_pass(pair[:, c, :], codes[2], c, 4 + c, h, (h, c) == (SECOND, 0), (h, c) == (FIRST, 1))
         finish(0, early[0][:])
-        codes7 = at("codes7", [P, 2, P], U16, 5)
+        store(0, 1)
+        codes7 = at("codes7", [P, 2, P], U16, 10)
         part(codes7, words7)
         for c, last_codes in enumerate((codes6, codes7)):
             for h in (FIRST, SECOND):
                 one_pass(late[c][:, 0, :], last_codes, 0, 6 + c, h, h == FIRST, h == SECOND)
+        y_held = laid.tile([P, 5, M], F32, name="y_held", align_bytes=64, offset=10 * KIB + 4 * P)
         for t in range(1, 4):
-            finish(t, early[t][:])
-            if t % 2:
-                store(t - 1, 2)
-        finish(4, pair[:])
+            finish(t, early[t][:], y_held[:, t - 1 : t, :])
+            store(t, 1)
+        finish(4, pair[:], y_held[:, 3:5, :])
         store(4, 2)
         for c in range(2):
             finish(6 + c, late[c][:])

@@ -42,14 +42,13 @@ def tile_list_tab4_tm_silu_kernel(tc, tab, w, b, offs, out):
         w_raw = {FIRST: at("w_raw_first", [P, 4, M], F32, 0), SECOND: at("w_raw_second", [P, 4, M], F32, 3)}
         w_codes = [held.tile([P, M], U32, name=f"w_codes{h}", align_bytes=64) for h in range(2)]
         w_scales = [held.tile([P, M], U8, name=f"w_scales{h}", align_bytes=64) for h in range(2)]
-        b_line = held.tile([1, M], F32, name="b_line")
         b_square = held.tile([P, M], F32, name="b_square", align_bytes=64)
         b_col = laid.tile([P, 2, 16], F32, name="b_col", align_bytes=64, offset=8 * KIB - 64)
         b_row = held.tile([P, M], F32, name="b_row", align_bytes=64)
         ident = held.tile([P, P], F32, name="ident", align_bytes=64)
         warm = held.tile([P, 1], F32, name="warm")
 
-        nc.scalar.dma_start(b_line[:], b.rearrange("(o n) -> o n", o=1))
+        nc.scalar.dma_start(b_square[P - 1 : P, :], b.rearrange("(o n) -> o n", o=1))
         scale_rows = tab[0, WORD_BYTES : WORD_BYTES + 32 * T].rearrange("(q t) -> q t", t=T)
         nc.sync.dma_start(scale_tab[0:32, :].bitcast(I32), scale_rows.bitcast(I32))
         nc.sync.dma_start(offsets[:], offs)
@@ -66,10 +65,9 @@ def tile_list_tab4_tm_silu_kernel(tc, tab, w, b, offs, out):
 
         make_identity(nc, ident[:])
         b_banks = psum.tile([P, 7, BANK // 4], F32, name="b_banks", offset=0)
-        nc.gpsimd.memset(b_square[:], 0.0)
-        nc.scalar.copy(b_square[0:1, :], b_line[:])
+        nc.gpsimd.memset(b_square[0 : P - 1, :], 0.0)
         nc.tensor.transpose(b_banks[:, 0, 0:P], b_square[:], ident[:])
-        nc.scalar.copy(b_col[:, 0, 0:1], b_banks[:, 0, 0:1])
+        nc.scalar.copy(b_col[:, 0, 0:1], b_banks[:, 0, P - 1 : P])
         b_spread = psum.tile([P, M], F32, name="b_spread", offset=7 * BANK)
         nc.tensor.transpose(b_spread[:], b_col[:, 0, 0:1].to_broadcast([P, M]), ident[:])
         nc.scalar.copy(b_row[:], b_spread[:])
@@ -135,15 +133,15 @@ def tile_list_tab4_tm_silu_kernel(tc, tab, w, b, offs, out):
 
         words = [held.tile([P, CHUNK], U32, name=f"words{s}", align_bytes=64) for s in range(2)]
         words.append(laid.tile([P, CHUNK], U32, name="words2", align_bytes=64, offset=KIB + S - HALF))
-        codes = [at("codes0", [P, 2, CHUNK], U16, 5), laid.tile([P, 2, CHUNK], U16, name="codes1", align_bytes=64, offset=S - HALF), at("codes2", [P, 2, CHUNK], U16, 3)]
+        codes = [at("codes0", [P, 2, CHUNK], U16, 5), held.tile([P, 2, CHUNK], U16, name="codes1", align_bytes=64), at("codes2", [P, 2, CHUNK], U16, 3)]
         words6 = at("words6", [P, P], U32, 4)
         words7 = laid.tile([P, P], U32, name="words7", align_bytes=64, offset=4 * KIB + 4 * P)
         codes6 = held.tile([P, 2, P], U16, name="codes6", align_bytes=64)
         gather(words[0], 0)
         gather(words[1], 2)
         part(codes[0], words[0])
-        quantize(FIRST)
         part(codes[1], words[1])
+        quantize(FIRST)
         gather(words[2], 4)
         nc.vector.tensor_copy(live(first_late, 0), rows(FIRST, 0, HALF, S))
         quantize(SECOND)

@@ -18,11 +18,11 @@ ADD = mybir.AluOpType.add
 
 P = 128
 WORD_BYTES = 512 * T
-CHUNK = 256
 KIB = 1024
 BANK = 2048
 FIRST, SECOND = 0, 1
-HALF = 3 * S // 4
+TILES = S // P
+EARLY = 3 * S // 4
 
 
 def tile_list_tab4_tm_silu_kernel(tc, tab, w, b, offs, out):
@@ -32,32 +32,32 @@ def tile_list_tab4_tm_silu_kernel(tc, tab, w, b, offs, out):
         tc.tile_pool(name="laid", bufs=1) as laid,
         tc.psum_pool(name="psum", bufs=1) as psum,
     ):
-        def at(name, shape, dtype, kib):
-            return laid.tile(shape, dtype, name=name, align_bytes=64, offset=kib * KIB)
+        def at(name, shape, dtype, byte):
+            return laid.tile(shape, dtype, name=name, align_bytes=64, offset=byte)
+
+        def own(name, shape, dtype):
+            return held.tile(shape, dtype, name=name, align_bytes=64)
 
         offsets = held.tile([P, S // 16], U16, name="offsets")
-        scale_tab = held.tile([P, T], U8, name="scale_tab", align_bytes=64)
-        word_tab = held.tile([P, T], I32, name="word_tab", align_bytes=64)
-        picked = at("picked", [P, S], U8, 10)
-        w_raw = {FIRST: at("w_raw_first", [P, 4, M], F32, 0), SECOND: at("w_raw_second", [P, 4, M], F32, 3)}
-        w_codes = [held.tile([P, M], U32, name=f"w_codes{h}", align_bytes=64) for h in range(2)]
-        w_scales = [held.tile([P, M], U8, name=f"w_scales{h}", align_bytes=64) for h in range(2)]
-        b_square = held.tile([P, M], F32, name="b_square", align_bytes=64)
-        b_col = laid.tile([P, 2, 16], F32, name="b_col", align_bytes=64, offset=8 * KIB - 64)
-        b_row = held.tile([P, M], F32, name="b_row", align_bytes=64)
-        ident = held.tile([P, P], F32, name="ident", align_bytes=64)
+        scale_tab = own("scale_tab", [P, T], U8)
+        word_tab = own("word_tab", [P, T], I32)
+        picked = own("picked", [P, S], U8)
+        w_raw = [at("w_raw0", [P, 4, M], F32, KIB), at("w_raw1", [P, 4, M], F32, 4 * KIB)]
+        w_codes = [own(f"w_codes{h}", [P, M], U32) for h in range(2)]
+        w_scales = [own(f"w_scales{h}", [P, M], U8) for h in range(2)]
+        b_square = own("b_square", [P, M], F32)
+        b_col = at("b_col", [P, 2, 16], F32, 8 * KIB - 64)
+        b_row = own("b_row", [P, M], F32)
+        ident = own("ident", [P, P], F32)
         warm = held.tile([P, 1], F32, name="warm")
 
         nc.scalar.dma_start(b_square[P - 1 : P, :], b.rearrange("(o n) -> o n", o=1))
         scale_rows = tab[0, WORD_BYTES : WORD_BYTES + 32 * T].rearrange("(q t) -> q t", t=T)
         nc.sync.dma_start(scale_tab[0:32, :].bitcast(I32), scale_rows.bitcast(I32))
         nc.sync.dma_start(offsets[:], offs)
-        def load_w(h):
-            nc.sync.dma_start(w_raw[h][:].rearrange("p i n -> p (i n)"), w[512 * h : 512 * (h + 1), :].rearrange("(p i) n -> p (i n)", i=4))
-
         nc.sync.dma_start(word_tab[:], tab[0, 0:WORD_BYTES].rearrange("(p x) -> p x", p=P).bitcast(I32))
-        load_w(FIRST)
-        load_w(SECOND)
+        for h in (FIRST, SECOND):
+            nc.sync.dma_start(w_raw[h][:].rearrange("p i n -> p (i n)"), w[512 * h : 512 * (h + 1), :].rearrange("(p i) n -> p (i n)", i=4))
         nc.vector.memset(scale_tab[32:64, :].bitcast(I32), 0)
         nc.vector.memset(scale_tab[64:128, :].bitcast(I32), 0)
         nc.vector.memset(warm[:], 0.0)
@@ -72,7 +72,15 @@ def tile_list_tab4_tm_silu_kernel(tc, tab, w, b, offs, out):
         nc.tensor.transpose(b_spread[:], b_col[:, 0, 0:1].to_broadcast([P, M]), ident[:])
         nc.scalar.copy(b_row[:], b_spread[:])
 
-        w_grp = {FIRST: at("w_grp_first", [P, M, 4], BF16, 7), SECOND: at("w_grp_second", [P, M, 4], BF16, 8)}
+        w_grp = [at("w_grp0", [P, M, 4], BF16, 7 * KIB), at("w_grp1", [P, M, 4], BF16, 8 * KIB)]
+        first_early = own("first_early", [P, EARLY], U8)
+        first_late = at("first_late", [P, S - EARLY], U8, KIB + 256)
+        second = own("second", [P, S], U8)
+
+        def plane(h, t):
+            if h == SECOND:
+                return second[:, t * P : (t + 1) * P]
+            return first_early[:, t * P : (t + 1) * P] if t * P < EARLY else first_late[:, t * P - EARLY : (t + 1) * P - EARLY]
 
         def round_w(h):
             nc.scalar.activation(w_grp[h][:].rearrange("p (c j) i -> p c i j", j=4), w_raw[h][:].rearrange("p i (c j) -> p c i j", j=4), COPY)
@@ -84,20 +92,19 @@ def tile_list_tab4_tm_silu_kernel(tc, tab, w, b, offs, out):
             n = words.shape[1]
             nc.vector.tensor_copy(words[:], word_tab[:].bitcast(U32).indirect(offsets[:, t0 * P // 16 : (t0 * P + n) // 16]))
 
-        def part(codes, words):
-            nc.vector.tensor_copy(codes[:], words[:].bitcast(U16).rearrange("p (t h) -> p h t", h=2))
+        def part(codes, words, c0):
+            n = codes.shape[2]
+            nc.vector.tensor_copy(codes[:], words[:, c0 : c0 + n].bitcast(U16).rearrange("p (t h) -> p h t", h=2))
 
-        def one_pass(acc, codes, c, t, h, start, stop):
+        def one_pass(t, codes, c, h, start):
             raw = codes[:].rearrange("p h t -> p (h t)").bitcast(U8)
             b0 = 2 * (h * codes.shape[2] + c * P)
-            nc.tensor.matmul_mx(out=acc, lhsT=raw[:, b0 : b0 + 2 * P].bitcast(FP4X4), lhsT_scale=plane(h, t),
-                                rhs=w_codes[h][:].bitcast(FP8X4), rhs_scale=w_scales[h][:], start=start, stop=stop)
+            nc.tensor.matmul_mx(out=acc[t][:], lhsT=raw[:, b0 : b0 + 2 * P].bitcast(FP4X4), lhsT_scale=plane(h, t),
+                                rhs=w_codes[h][:].bitcast(FP8X4), rhs_scale=w_scales[h][:], start=start, stop=not start)
 
-        def finish(t, acc, y=None):
-            n = acc.shape[1]
-            y = y if y is not None else held.tile([P, n, M], F32, name=f"y{t}", align_bytes=64)[:]
-            nc.vector.tensor_tensor(y, acc, b_row[:].unsqueeze(1).to_broadcast([P, n, M]), ADD)
-            nc.scalar.activation(o[:, t : t + n, :], y, SILU)
+        def finish(t):
+            nc.vector.tensor_tensor(y[:, t, :], acc[t][:], b_row[:], ADD)
+            nc.scalar.activation(o[:, t, :], y[:, t, :], SILU)
 
         def store(t0, n):
             nc.sync.dma_start(out[t0 * P : (t0 + n) * P, :].rearrange("(c p) n -> p c n", p=P), o[:, t0 : t0 + n, :])
@@ -108,71 +115,60 @@ def tile_list_tab4_tm_silu_kernel(tc, tab, w, b, offs, out):
         def rows(h, q, c0, c1):
             return picked[16 * h + 4 * q : 16 * h + 4 * q + 4, c0:c1].bitcast(I32)
 
-        def live(plane, q):
-            return plane[32 * q : 32 * q + 4, :].bitcast(I32)
+        def live(tile, q):
+            return tile[32 * q : 32 * q + 4, :].bitcast(I32)
 
         round_w(FIRST)
-        first_early = held.tile([P, HALF], U8, name="first_early", align_bytes=64)
-        second = held.tile([P, S], U8, name="second", align_bytes=64)
-        pick(0, HALF)
+        round_w(SECOND)
+        pick(0, EARLY)
         for q in range(1, 4):
-            nc.sync.dma_start(live(first_early, q), rows(FIRST, q, 0, HALF))
-        pick(HALF, S)
-        nc.vector.tensor_copy(live(first_early, 0), rows(FIRST, 0, 0, HALF))
+            nc.sync.dma_start(live(first_early, q), rows(FIRST, q, 0, EARLY))
+        pick(EARLY, S)
+        nc.vector.tensor_copy(live(first_early, 0), rows(FIRST, 0, 0, EARLY))
         for q in range(4):
             nc.sync.dma_start(live(second, q), rows(SECOND, q, 0, S))
-        first_late = at("first_late", [P, S - HALF], U8, 0)
         for q in range(1, 4):
-            nc.sync.dma_start(live(first_late, q), rows(FIRST, q, HALF, S))
-        round_w(SECOND)
+            nc.sync.dma_start(live(first_late, q), rows(FIRST, q, EARLY, S))
 
-        def plane(h, t):
-            if h == SECOND:
-                return second[:, t * P : (t + 1) * P]
-            return first_early[:, t * P : (t + 1) * P] if t * P < HALF else first_late[:, t * P - HALF : (t + 1) * P - HALF]
-
-        words = [held.tile([P, CHUNK], U32, name=f"words{s}", align_bytes=64) for s in range(2)]
-        words.append(laid.tile([P, CHUNK], U32, name="words2", align_bytes=64, offset=KIB + S - HALF))
-        codes = [at("codes0", [P, 2, CHUNK], U16, 5), held.tile([P, 2, CHUNK], U16, name="codes1", align_bytes=64), at("codes2", [P, 2, CHUNK], U16, 3)]
-        words6 = at("words6", [P, P], U32, 4)
-        words7 = laid.tile([P, P], U32, name="words7", align_bytes=64, offset=4 * KIB + 4 * P)
-        codes6 = held.tile([P, 2, P], U16, name="codes6", align_bytes=64)
-        gather(words[0], 0)
-        gather(words[1], 2)
-        part(codes[0], words[0])
-        part(codes[1], words[1])
+        words_a = own("words_a", [P, 4 * P], U32)
+        words_b = at("words_b", [P, 2 * P], U32, KIB + 512)
+        words_c = at("words_c", [P, 2 * P], U32, 8 * KIB)
+        codes01 = at("codes01", [P, 2, 2 * P], U16, 256)
+        codes23 = at("codes23", [P, 2, 2 * P], U16, 5 * KIB)
+        codes45 = at("codes45", [P, 2, 2 * P], U16, 4 * KIB)
+        gather(words_a, 0)
         quantize(FIRST)
-        gather(words[2], 4)
-        nc.vector.tensor_copy(live(first_late, 0), rows(FIRST, 0, HALF, S))
+        part(codes01, words_a, 0)
+        gather(words_b, 4)
+        nc.vector.tensor_copy(live(first_late, 0), rows(FIRST, 0, EARLY, S))
         quantize(SECOND)
-        gather(words6, 6)
-        part(codes[2], words[2])
-        gather(words7, 7)
-        part(codes6, words6)
+        part(codes23, words_a, 2 * P)
+        part(codes45, words_b, 0)
+        gather(words_c, 6)
 
-        o = held.tile([P, S // P, M], F32, name="o", align_bytes=64)
-        early = [psum.tile([P, 1, M], F32, name=f"early{t}", offset=BANK * t) for t in range(4)]
-        pair = psum.tile([P, 2, M], F32, name="pair", offset=BANK * 4)
-        late = [psum.tile([P, 1, M], F32, name=f"late{c}", offset=BANK * (5 + c)) for c in range(2)]
+        y = own("y", [P, TILES, M], F32)
+        o = own("o", [P, TILES, M], F32)
+        acc = [psum.tile([P, M], F32, name=f"acc{t}", offset=BANK * t) for t in range(TILES)]
         for h in (FIRST, SECOND):
-            for t in range(4):
-                one_pass(early[t][:, 0, :], codes[t // 2], t % 2, t, h, h == FIRST, h == SECOND)
-        for h in (SECOND, FIRST):
             for c in range(2):
-                one_pass(pair[:, c, :], codes[2], c, 4 + c, h, (h, c) == (SECOND, 0), (h, c) == (FIRST, 1))
-        finish(0, early[0][:])
-        store(0, 1)
-        codes7 = at("codes7", [P, 2, P], U16, 10)
-        part(codes7, words7)
-        for c, last_codes in enumerate((codes6, codes7)):
-            for h in (FIRST, SECOND):
-                one_pass(late[c][:, 0, :], last_codes, 0, 6 + c, h, h == FIRST, h == SECOND)
-        y_held = laid.tile([P, 5, M], F32, name="y_held", align_bytes=64, offset=10 * KIB + 4 * P)
-        for t in range(1, 4):
-            finish(t, early[t][:], y_held[:, t - 1 : t, :])
+                one_pass(c, codes01, c, h, h == FIRST)
+        for t0, codes in ((2, codes23), (4, codes45)):
+            for h in (SECOND, FIRST):
+                for c in range(2):
+                    one_pass(t0 + c, codes, c, h, h == SECOND)
+        finish(0)
+        finish(1)
+        store(0, 2)
+        codes6 = at("codes6", [P, 2, P], U16, 256)
+        part(codes6, words_c, 0)
+        for h in (FIRST, SECOND):
+            one_pass(6, codes6, 0, h, h == FIRST)
+        finish(2)
+        store(2, 1)
+        codes7 = at("codes7", [P, 2, P], U16, 5 * KIB)
+        part(codes7, words_c, P)
+        for h in (FIRST, SECOND):
+            one_pass(7, codes7, 0, h, h == FIRST)
+        for t in range(3, TILES):
+            finish(t)
             store(t, 1)
-        finish(4, pair[:], y_held[:, 3:5, :])
-        store(4, 2)
-        for c in range(2):
-            finish(6 + c, late[c][:])
-            store(6 + c, 1)

@@ -74,7 +74,7 @@ def tile_list_tab4_tm_silu_kernel(tc, tab, w, b, offs, out):
 
         w_grp = [at("w_grp0", [P, M, 4], BF16, 7 * KIB), at("w_grp1", [P, M, 4], BF16, 8 * KIB)]
         first_early = own("first_early", [P, EARLY], U8)
-        first_late = at("first_late", [P, S - EARLY], U8, KIB + 256)
+        first_late = at("first_late", [P, S - EARLY], U8, 2 * KIB + 512)
         second = own("second", [P, S], U8)
 
         def plane(h, t):
@@ -96,15 +96,16 @@ def tile_list_tab4_tm_silu_kernel(tc, tab, w, b, offs, out):
             n = codes.shape[2]
             nc.vector.tensor_copy(codes[:], words[:, c0 : c0 + n].bitcast(U16).rearrange("p (t h) -> p h t", h=2))
 
-        def one_pass(t, codes, c, h, start):
+        def one_pass(t, codes, c, h, start, stop):
             raw = codes[:].rearrange("p h t -> p (h t)").bitcast(U8)
             b0 = 2 * (h * codes.shape[2] + c * P)
-            nc.tensor.matmul_mx(out=acc[t][:], lhsT=raw[:, b0 : b0 + 2 * P].bitcast(FP4X4), lhsT_scale=plane(h, t),
-                                rhs=w_codes[h][:].bitcast(FP8X4), rhs_scale=w_scales[h][:], start=start, stop=not start)
+            nc.tensor.matmul_mx(out=acc[t], lhsT=raw[:, b0 : b0 + 2 * P].bitcast(FP4X4), lhsT_scale=plane(h, t),
+                                rhs=w_codes[h][:].bitcast(FP8X4), rhs_scale=w_scales[h][:], start=start, stop=stop)
 
-        def finish(t):
-            nc.vector.tensor_tensor(y[:, t, :], acc[t][:], b_row[:], ADD)
-            nc.scalar.activation(o[:, t, :], y[:, t, :], SILU)
+        def finish(t0, bank, y):
+            n = bank.shape[1]
+            nc.vector.tensor_tensor(y, bank[:], b_row[:].unsqueeze(1).to_broadcast([P, n, M]), ADD)
+            nc.scalar.activation(o[:, t0 : t0 + n, :], y, SILU)
 
         def store(t0, n):
             nc.sync.dma_start(out[t0 * P : (t0 + n) * P, :].rearrange("(c p) n -> p c n", p=P), o[:, t0 : t0 + n, :])
@@ -127,48 +128,50 @@ def tile_list_tab4_tm_silu_kernel(tc, tab, w, b, offs, out):
         nc.vector.tensor_copy(live(first_early, 0), rows(FIRST, 0, 0, EARLY))
         for q in range(4):
             nc.sync.dma_start(live(second, q), rows(SECOND, q, 0, S))
-        for q in range(1, 4):
+        for q in range(4):
             nc.sync.dma_start(live(first_late, q), rows(FIRST, q, EARLY, S))
 
         words_a = own("words_a", [P, 4 * P], U32)
-        words_b = at("words_b", [P, 2 * P], U32, KIB + 512)
-        words_c = at("words_c", [P, 2 * P], U32, 8 * KIB)
+        words_b = at("words_b", [P, 2 * P], U32, 4 * KIB)
+        words6 = at("words6", [P, P], U32, 5 * KIB)
         codes01 = at("codes01", [P, 2, 2 * P], U16, 256)
-        codes23 = at("codes23", [P, 2, 2 * P], U16, 5 * KIB)
-        codes45 = at("codes45", [P, 2, 2 * P], U16, 4 * KIB)
+        codes23 = at("codes23", [P, 2, 2 * P], U16, KIB + 512)
+        codes4 = own("codes4", [P, 2, P], U16)
+        codes5 = own("codes5", [P, 2, P], U16)
         gather(words_a, 0)
         quantize(FIRST)
         part(codes01, words_a, 0)
-        gather(words_b, 4)
-        nc.vector.tensor_copy(live(first_late, 0), rows(FIRST, 0, EARLY, S))
-        quantize(SECOND)
         part(codes23, words_a, 2 * P)
-        part(codes45, words_b, 0)
-        gather(words_c, 6)
+        quantize(SECOND)
+        gather(words_b, 4)
+        gather(words6, 6)
+        part(codes4, words_b, 0)
+        part(codes5, words_b, P)
 
-        y = own("y", [P, TILES, M], F32)
         o = own("o", [P, TILES, M], F32)
-        acc = [psum.tile([P, M], F32, name=f"acc{t}", offset=BANK * t) for t in range(TILES)]
+        banks = {t: psum.tile([P, 2 if t == 4 else 1, M], F32, name=f"bank{t}", offset=BANK * t) for t in (0, 1, 2, 3, 4, 6, 7)}
+        acc = [banks[4][:, 1, :] if t == 5 else banks[t][:, 0, :] for t in range(TILES)]
         for h in (FIRST, SECOND):
-            for c in range(2):
-                one_pass(c, codes01, c, h, h == FIRST)
-        for t0, codes in ((2, codes23), (4, codes45)):
+            for t in range(4):
+                one_pass(t, (codes01, codes23)[t // 2], t % 2, h, h == FIRST, h == SECOND)
+        for t, codes in ((4, codes4), (5, codes5)):
             for h in (SECOND, FIRST):
-                for c in range(2):
-                    one_pass(t0 + c, codes, c, h, h == SECOND)
-        finish(0)
-        finish(1)
-        store(0, 2)
-        codes6 = at("codes6", [P, 2, P], U16, 256)
-        part(codes6, words_c, 0)
+                one_pass(t, codes, 0, h, (t, h) == (4, SECOND), (t, h) == (5, FIRST))
+        words7 = at("words7", [P, P], U32, 0)
+        codes6 = at("codes6", [P, 2, P], U16, 512)
+        y0 = at("y0", [P, 1, M], F32, KIB)
+        codes7 = own("codes7", [P, 2, P], U16)
+        y = own("y", [P, TILES - 1, M], F32)
+        gather(words7, 7)
+        part(codes6, words6, 0)
         for h in (FIRST, SECOND):
-            one_pass(6, codes6, 0, h, h == FIRST)
-        finish(2)
-        store(2, 1)
-        codes7 = at("codes7", [P, 2, P], U16, 5 * KIB)
-        part(codes7, words_c, P)
+            one_pass(6, codes6, 0, h, h == FIRST, h == SECOND)
+        finish(0, banks[0], y0[:])
+        store(0, 1)
+        part(codes7, words7, 0)
         for h in (FIRST, SECOND):
-            one_pass(7, codes7, 0, h, h == FIRST)
-        for t in range(3, TILES):
-            finish(t)
-            store(t, 1)
+            one_pass(7, codes7, 0, h, h == FIRST, h == SECOND)
+        for t in (1, 2, 3, 4, 6, 7):
+            n = banks[t].shape[1]
+            finish(t, banks[t], y[:, t - 1 : t - 1 + n, :])
+            store(t, n)

@@ -131,17 +131,19 @@ def tile_list_tab4_tm_silu_kernel(tc, tab, w, b, offs, out):
         for q in range(4):
             nc.sync.dma_start(live(first_late, q), rows(FIRST, q, EARLY, S))
 
-        words_a = own("words_a", [P, 4 * P], U32)
+        words01 = own("words01", [P, 2 * P], U32)
+        words23 = own("words23", [P, 2 * P], U32)
         words_b = at("words_b", [P, 2 * P], U32, 4 * KIB)
         words6 = at("words6", [P, P], U32, 5 * KIB)
-        codes01 = at("codes01", [P, 2, 2 * P], U16, 256)
+        codes01 = at("codes01", [P, 2, 2 * P], U16, 10 * KIB)
         codes23 = at("codes23", [P, 2, 2 * P], U16, KIB + 512)
         codes4 = own("codes4", [P, 2, P], U16)
         codes5 = own("codes5", [P, 2, P], U16)
-        gather(words_a, 0)
+        gather(words01, 0)
+        gather(words23, 2)
+        part(codes01, words01, 0)
         quantize(FIRST)
-        part(codes01, words_a, 0)
-        part(codes23, words_a, 2 * P)
+        part(codes23, words23, 0)
         quantize(SECOND)
         gather(words_b, 4)
         gather(words6, 6)
@@ -157,9 +159,9 @@ def tile_list_tab4_tm_silu_kernel(tc, tab, w, b, offs, out):
         for t, codes in ((4, codes4), (5, codes5)):
             for h in (SECOND, FIRST):
                 one_pass(t, codes, 0, h, (t, h) == (4, SECOND), (t, h) == (5, FIRST))
-        words7 = at("words7", [P, P], U32, 0)
-        codes6 = at("codes6", [P, 2, P], U16, 512)
-        y0 = at("y0", [P, 1, M], F32, KIB)
+        words7 = at("words7", [P, P], U32, 10 * KIB - 256)
+        codes6 = at("codes6", [P, 2, P], U16, 10 * KIB + 256)
+        y0 = at("y0", [P, 1, M], F32, 10 * KIB + 768)
         codes7 = own("codes7", [P, 2, P], U16)
         y = own("y", [P, TILES - 1, M], F32)
         gather(words7, 7)

@@ -33,12 +33,12 @@ def tile_list_tab4_tm_silu_kernel(tc, tab, w, b, offs, out):
         tc.psum_pool(name="psum", bufs=1) as psum,
     ):
         def at(name, shape, dtype, byte):
-            return laid.tile(shape, dtype, name=name, align_bytes=64, offset=byte)
+            return laid.tile(shape, dtype, name=name, align_bytes=64 if byte % 256 else 256, offset=byte)
 
         def own(name, shape, dtype):
-            return held.tile(shape, dtype, name=name, align_bytes=64)
+            return held.tile(shape, dtype, name=name, align_bytes=256)
 
-        offsets = held.tile([P, S // 16], U16, name="offsets")
+        offsets = own("offsets", [P, S // 16], U16)
         scale_tab = own("scale_tab", [P, T], U8)
         word_tab = own("word_tab", [P, T], I32)
         picked = own("picked", [P, S], U8)
@@ -133,47 +133,45 @@ def tile_list_tab4_tm_silu_kernel(tc, tab, w, b, offs, out):
 
         words01 = own("words01", [P, 2 * P], U32)
         words23 = own("words23", [P, 2 * P], U32)
-        words_b = at("words_b", [P, 2 * P], U32, 4 * KIB)
-        words6 = at("words6", [P, P], U32, 5 * KIB)
+        words45 = at("words45", [P, 2 * P], U32, KIB)
+        words6 = at("words6", [P, P], U32, 4 * KIB)
+        words7 = at("words7", [P, P], U32, 4 * KIB + 512)
         codes01 = at("codes01", [P, 2, 2 * P], U16, 10 * KIB)
-        codes23 = at("codes23", [P, 2, 2 * P], U16, KIB + 512)
-        codes4 = own("codes4", [P, 2, P], U16)
-        codes5 = own("codes5", [P, 2, P], U16)
+        codes23 = own("codes23", [P, 2, 2 * P], U16)
+        codes45 = at("codes45", [P, 2, 2 * P], U16, 5 * KIB)
         gather(words01, 0)
         gather(words23, 2)
         part(codes01, words01, 0)
-        quantize(FIRST)
         part(codes23, words23, 0)
+        quantize(FIRST)
+        gather(words45, 4)
         quantize(SECOND)
-        gather(words_b, 4)
         gather(words6, 6)
-        part(codes4, words_b, 0)
-        part(codes5, words_b, P)
+        part(codes45, words45, 0)
+        gather(words7, 7)
 
         o = own("o", [P, TILES, M], F32)
-        banks = {t: psum.tile([P, 2 if t == 4 else 1, M], F32, name=f"bank{t}", offset=BANK * t) for t in (0, 1, 2, 3, 4, 6, 7)}
-        acc = [banks[4][:, 1, :] if t == 5 else banks[t][:, 0, :] for t in range(TILES)]
+        pieces = ((0, 1), (1, 1), (2, 1), (3, 1), (4, 2), (6, 1), (7, 1))
+        banks = {t0: psum.tile([P, n, M], F32, name=f"bank{t0}", offset=BANK * t0) for t0, n in pieces}
+        acc = [banks[t0][:, c, :] for t0, n in pieces for c in range(n)]
+        opens = [c == 0 for t0, n in pieces for c in range(n)]
+        closes = [c == n - 1 for t0, n in pieces for c in range(n)]
         for h in (FIRST, SECOND):
             for t in range(4):
-                one_pass(t, (codes01, codes23)[t // 2], t % 2, h, h == FIRST, h == SECOND)
-        for t, codes in ((4, codes4), (5, codes5)):
-            for h in (SECOND, FIRST):
-                one_pass(t, codes, 0, h, (t, h) == (4, SECOND), (t, h) == (5, FIRST))
-        words7 = at("words7", [P, P], U32, 10 * KIB - 256)
-        codes6 = at("codes6", [P, 2, P], U16, 10 * KIB + 256)
-        y0 = at("y0", [P, 1, M], F32, 10 * KIB + 768)
-        codes7 = own("codes7", [P, 2, P], U16)
-        y = own("y", [P, TILES - 1, M], F32)
-        gather(words7, 7)
+                one_pass(t, (codes01, codes23)[t // 2], t % 2, h, h == FIRST and opens[t], h == SECOND and closes[t])
+        for h in (SECOND, FIRST):
+            for t in (4, 5):
+                one_pass(t, codes45, t % 2, h, h == SECOND and opens[t], h == FIRST and closes[t])
+        codes6 = at("codes6", [P, 2, P], U16, 10 * KIB - 256)
+        codes7 = at("codes7", [P, 2, P], U16, 10 * KIB + 256)
+        y = at("y", [P, TILES, M], F32, 10 * KIB + 768)
         part(codes6, words6, 0)
         for h in (FIRST, SECOND):
             one_pass(6, codes6, 0, h, h == FIRST, h == SECOND)
-        finish(0, banks[0], y0[:])
-        store(0, 1)
-        part(codes7, words7, 0)
-        for h in (FIRST, SECOND):
-            one_pass(7, codes7, 0, h, h == FIRST, h == SECOND)
-        for t in (1, 2, 3, 4, 6, 7):
-            n = banks[t].shape[1]
-            finish(t, banks[t], y[:, t - 1 : t - 1 + n, :])
-            store(t, n)
+        for t0, n in pieces:
+            finish(t0, banks[t0], y[:, t0 : t0 + n, :])
+            store(t0, n)
+            if t0 == 0:
+                part(codes7, words7, 0)
+                for h in (FIRST, SECOND):
+                    one_pass(7, codes7, 0, h, h == FIRST, h == SECOND)

@@ -136,8 +136,8 @@ def tile_list_tab4_tm_silu_kernel(tc, tab, w, b, offs, out):
         words45 = at("words45", [P, 2 * P], U32, KIB)
         words6 = at("words6", [P, P], U32, 4 * KIB)
         words7 = at("words7", [P, P], U32, 4 * KIB + 512)
-        codes01 = at("codes01", [P, 2, 2 * P], U16, 10 * KIB)
-        codes23 = own("codes23", [P, 2, 2 * P], U16)
+        codes01 = at("codes01", [P, 2, 2 * P], U16, 6 * KIB)
+        codes23 = at("codes23", [P, 2, 2 * P], U16, 10 * KIB)
         codes45 = at("codes45", [P, 2, 2 * P], U16, 5 * KIB)
         gather(words01, 0)
         gather(words23, 2)
@@ -162,16 +162,17 @@ def tile_list_tab4_tm_silu_kernel(tc, tab, w, b, offs, out):
         for h in (SECOND, FIRST):
             for t in (4, 5):
                 one_pass(t, codes45, t % 2, h, h == SECOND and opens[t], h == FIRST and closes[t])
-        codes6 = at("codes6", [P, 2, P], U16, 10 * KIB - 256)
-        codes7 = at("codes7", [P, 2, P], U16, 10 * KIB + 256)
-        y = at("y", [P, TILES, M], F32, 10 * KIB + 768)
+        codes6 = at("codes6", [P, 2, P], U16, 6 * KIB)
+        y01 = at("y01", [P, 2, M], F32, 6 * KIB + 512)
+        codes7 = at("codes7", [P, 2, P], U16, 10 * KIB)
+        y = at("y", [P, TILES - 2, M], F32, 10 * KIB + 512)
         part(codes6, words6, 0)
         for h in (FIRST, SECOND):
             one_pass(6, codes6, 0, h, h == FIRST, h == SECOND)
         for t0, n in pieces:
-            finish(t0, banks[t0], y[:, t0 : t0 + n, :])
+            finish(t0, banks[t0], y[:, t0 - 2 : t0 - 2 + n, :] if t0 > 1 else y01[:, t0 : t0 + 1, :])
             store(t0, n)
-            if t0 == 0:
+            if t0 == 1:
                 part(codes7, words7, 0)
                 for h in (FIRST, SECOND):
                     one_pass(7, codes7, 0, h, h == FIRST, h == SECOND)

@@ -94,7 +94,7 @@ def tile_list_tab4_tm_silu_kernel(tc, tab, w, b, offs, out):
 
         def part(codes, words, c0):
             n = codes.shape[2]
-            nc.vector.tensor_copy(codes[:], words[:, c0 : c0 + n].bitcast(U16).rearrange("p (t h) -> p h t", h=2))
+            nc.vector.tensor_copy(codes[:].rearrange("p h (u t) -> p u h t", u=2), words[:, c0 : c0 + n].bitcast(U16).rearrange("p (u t h) -> p u h t", u=2, h=2))
 
         def one_pass(t, codes, c, h, start, stop):
             raw = codes[:].rearrange("p h t -> p (h t)").bitcast(U8)

import concourse.mybir as mybir
from concourse.masks import make_identity

K, M, T, S = 1024, 128, 2048, 1024
FLOPS = 2 * K * M * S

F32 = mybir.dt.float32
BF16 = mybir.dt.bfloat16
I32 = mybir.dt.int32
U32 = mybir.dt.uint32
U16 = mybir.dt.uint16
U8 = mybir.dt.uint8
FP8X4 = mybir.dt.float8_e4m3fn_x4
FP4X4 = mybir.dt.float4_e2m1fn_x4
SILU = mybir.ActivationFunctionType.Silu
COPY = mybir.ActivationFunctionType.Copy
ADD = mybir.AluOpType.add

P = 128
WORD_BYTES = 512 * T
KIB = 1024
BANK = 2048
FIRST, SECOND = 0, 1
TILES = S // P
EARLY = 3 * S // 4


def tile_list_tab4_tm_silu_kernel(tc, tab, w, b, offs, out):
    nc = tc.nc
    with (
        tc.tile_pool(name="held", bufs=1) as held,
        tc.tile_pool(name="laid", bufs=1) as laid,
        tc.psum_pool(name="psum", bufs=1) as psum,
    ):
        def at(name, shape, dtype, byte):
            return laid.tile(shape, dtype, name=name, align_bytes=64 if byte % 256 else 256, offset=byte)

        def own(name, shape, dtype):
            return held.tile(shape, dtype, name=name, align_bytes=256)

        offsets = own("offsets", [P, S // 16], U16)
        scale_tab = own("scale_tab", [P, T], U8)
        word_tab = own("word_tab", [P, T], I32)
        picked = own("picked", [P, S], U8)
        w_raw = [at("w_raw0", [P, 4, M], F32, KIB), at("w_raw1", [P, 4, M], F32, 4 * KIB)]
        w_codes = [own(f"w_codes{h}", [P, M], U32) for h in range(2)]
        w_scales = [own(f"w_scales{h}", [P, M], U8) for h in range(2)]
        b_square = own("b_square", [P, M], F32)
        b_col = at("b_col", [P, 2, 16], F32, 8 * KIB - 64)
        b_row = own("b_row", [P, M], F32)
        ident = own("ident", [P, P], F32)
        warm = held.tile([P, 1], F32, name="warm")

        nc.scalar.dma_start(b_square[P - 1 : P, :], b.rearrange("(o n) -> o n", o=1))
        scale_rows = tab[0, WORD_BYTES : WORD_BYTES + 32 * T].rearrange("(q t) -> q t", t=T)
        nc.sync.dma_start(scale_tab[0:32, :].bitcast(I32), scale_rows.bitcast(I32))
        nc.sync.dma_start(offsets[:], offs)
        nc.sync.dma_start(word_tab[:], tab[0, 0:WORD_BYTES].rearrange("(p x) -> p x", p=P).bitcast(I32))
        for h in (FIRST, SECOND):
            nc.sync.dma_start(w_raw[h][:].rearrange("p i n -> p (i n)"), w[512 * h : 512 * (h + 1), :].rearrange("(p i) n -> p (i n)", i=4))
        nc.vector.memset(scale_tab[32:64, :].bitcast(I32), 0)
        nc.vector.memset(scale_tab[64:128, :].bitcast(I32), 0)
        nc.vector.memset(warm[:], 0.0)
        nc.scalar.activation(warm[:], warm[:], SILU)

        make_identity(nc, ident[:])
        b_banks = psum.tile([P, 7, BANK // 4], F32, name="b_banks", offset=0)
        nc.gpsimd.memset(b_square[0 : P - 1, :], 0.0)
        nc.tensor.transpose(b_banks[:, 0, 0:P], b_square[:], ident[:])
        nc.scalar.copy(b_col[:, 0, 0:1], b_banks[:, 0, P - 1 : P])
        b_spread = psum.tile([P, M], F32, name="b_spread", offset=7 * BANK)
        nc.tensor.transpose(b_spread[:], b_col[:, 0, 0:1].to_broadcast([P, M]), ident[:])
        nc.scalar.copy(b_row[:], b_spread[:])

        w_grp = [at("w_grp0", [P, M, 4], BF16, 7 * KIB), at("w_grp1", [P, M, 4], BF16, 8 * KIB)]
        first_early = own("first_early", [P, EARLY], U8)
        first_late = at("first_late", [P, S - EARLY], U8, 2 * KIB + 512)
        second = own("second", [P, S], U8)

        def plane(h, t):
            if h == SECOND:
                return second[:, t * P : (t + 1) * P]
            return first_early[:, t * P : (t + 1) * P] if t * P < EARLY else first_late[:, t * P - EARLY : (t + 1) * P - EARLY]

        def round_w(h):
            nc.scalar.activation(w_grp[h][:].rearrange("p (c j) i -> p c i j", j=4), w_raw[h][:].rearrange("p i (c j) -> p c i j", j=4), COPY)

        def quantize(h):
            nc.vector.quantize_mx(out=w_codes[h][:].bitcast(FP8X4), scales=w_scales[h][:], in_=w_grp[h][:].rearrange("p n i -> p (n i)"))

        def gather(words, t0):
            n = words.shape[1]
            nc.vector.tensor_copy(words[:], word_tab[:].bitcast(U32).indirect(offsets[:, t0 * P // 16 : (t0 * P + n) // 16]))

        def part(codes, words, c0):
            n = codes.shape[2]
            nc.vector.tensor_copy(codes[:].rearrange("p h (u t) -> p u h t", u=2), words[:, c0 : c0 + n].bitcast(U16).rearrange("p (u t h) -> p u h t", u=2, h=2))

        def one_pass(t, codes, c, h, start, stop):
            raw = codes[:].rearrange("p h t -> p (h t)").bitcast(U8)
            b0 = 2 * (h * codes.shape[2] + c * P)
            nc.tensor.matmul_mx(out=acc[t], lhsT=raw[:, b0 : b0 + 2 * P].bitcast(FP4X4), lhsT_scale=plane(h, t),
                                rhs=w_codes[h][:].bitcast(FP8X4), rhs_scale=w_scales[h][:], start=start, stop=stop)

        def finish(t0, bank, y):
            n = bank.shape[1]
            nc.vector.tensor_tensor(y, bank[:], b_row[:].unsqueeze(1).to_broadcast([P, n, M]), ADD)
            nc.scalar.activation(o[:, t0 : t0 + n, :], y, SILU)

        def store(t0, n):
            nc.sync.dma_start(out[t0 * P : (t0 + n) * P, :].rearrange("(c p) n -> p c n", p=P), o[:, t0 : t0 + n, :])

        def pick(c0, c1):
            nc.vector.tensor_copy(picked[:, c0:c1], scale_tab[:].indirect(offsets[:, c0 // 16 : c1 // 16]))

        def rows(h, q, c0, c1):
            return picked[16 * h + 4 * q : 16 * h + 4 * q + 4, c0:c1].bitcast(I32)

        def live(tile, q):
            return tile[32 * q : 32 * q + 4, :].bitcast(I32)

        round_w(FIRST)
        round_w(SECOND)
        pick(0, EARLY)
        for q in range(1, 4):
            nc.sync.dma_start(live(first_early, q), rows(FIRST, q, 0, EARLY))
        pick(EARLY, S)
        nc.vector.tensor_copy(live(first_early, 0), rows(FIRST, 0, 0, EARLY))
        for q in range(4):
            nc.sync.dma_start(live(second, q), rows(SECOND, q, 0, S))
        for q in range(4):
            nc.sync.dma_start(live(first_late, q), rows(FIRST, q, EARLY, S))

        words01 = own("words01", [P, 2 * P], U32)
        words23 = own("words23", [P, 2 * P], U32)
        words45 = at("words45", [P, 2 * P], U32, KIB)
        words6 = at("words6", [P, P], U32, 4 * KIB)
        words7 = at("words7", [P, P], U32, 4 * KIB + 512)
        codes01 = at("codes01", [P, 2, 2 * P], U16, 6 * KIB)
        codes23 = at("codes23", [P, 2, 2 * P], U16, 10 * KIB)
        codes45 = at("codes45", [P, 2, 2 * P], U16, 5 * KIB)
        gather(words01, 0)
        gather(words23, 2)
        part(codes01, words01, 0)
        part(codes23, words23, 0)
        quantize(FIRST)
        gather(words45, 4)
        quantize(SECOND)
        gather(words6, 6)
        part(codes45, words45, 0)
        gather(words7, 7)

        o = own("o", [P, TILES, M], F32)
        pieces = ((0, 1), (1, 1), (2, 1), (3, 1), (4, 2), (6, 1), (7, 1))
        banks = {t0: psum.tile([P, n, M], F32, name=f"bank{t0}", offset=BANK * t0) for t0, n in pieces}
        acc = [banks[t0][:, c, :] for t0, n in pieces for c in range(n)]
        opens = [c == 0 for t0, n in pieces for c in range(n)]
        closes = [c == n - 1 for t0, n in pieces for c in range(n)]
        for h in (FIRST, SECOND):
            for t in range(4):
                one_pass(t, (codes01, codes23)[t // 2], t % 2, h, h == FIRST and opens[t], h == SECOND and closes[t])
        for h in (SECOND, FIRST):
            for t in (4, 5):
                one_pass(t, codes45, t % 2, h, h == SECOND and opens[t], h == FIRST and closes[t])
        codes6 = at("codes6", [P, 2, P], U16, 6 * KIB)
        y01 = at("y01", [P, 2, M], F32, 6 * KIB + 512)
        codes7 = at("codes7", [P, 2, P], U16, 10 * KIB)
        y = at("y", [P, TILES - 2, M], F32, 10 * KIB + 512)
        part(codes6, words6, 0)
        for h in (FIRST, SECOND):
            one_pass(6, codes6, 0, h, h == FIRST, h == SECOND)
        for t0, n in pieces:
            finish(t0, banks[t0], y[:, t0 - 2 : t0 - 2 + n, :] if t0 > 1 else y01[:, t0 : t0 + 1, :])
            store(t0, n)
            if t0 == 1:
                part(codes7, words7, 0)
                for h in (FIRST, SECOND):
                    one_pass(7, codes7, 0, h, h == FIRST, h == SECOND)
